import numpy as np, ml_dtypes
CORES = [10,34,74,98]
N = 4
import mx_ref
BF = ml_dtypes.bfloat16
def gentries(a):
    return np.ascontiguousarray(a.reshape(8, 16, -1).transpose(0, 2, 1)).reshape(8, -1)
def gtable(e):
    e = np.asarray(e); return np.ascontiguousarray(e.reshape(8, -1, 16).transpose(0, 2, 1)).reshape(128, -1).astype(np.int32)
def gcols(t, e):
    v = np.concatenate([t.reshape(8, 16, -1, 4), np.zeros((8, 16, 1, 4), BF)], axis=2)
    return np.ascontiguousarray(np.stack([v[g][:, e[g]] for g in range(8)])).reshape(128, -1)
def tile(rs):
    return np.stack(rs, axis=2).reshape(128, -1).astype(BF)
def cut(t, i, w=512):
    return t[:, w * i:w * i + w]
def pick(q, e):
    c = np.concatenate([q[0].reshape(128, -1, 4), np.zeros((128, 1, 4), np.uint8)], axis=1); s = np.concatenate([q[1], np.ones((16, 1), np.uint8)], axis=1)
    return (np.ascontiguousarray(c[:, e].reshape(128, -1)), np.ascontiguousarray(s[:, e]))
def join(*qs):
    return (np.concatenate([q[0] for q in qs], axis=1), np.concatenate([q[1] for q in qs], axis=1))
def put(q, e, v):
    c, s = q[0].reshape(128, -1, 4).copy(), q[1].copy(); c[:, e] = v[0].reshape(128, -1, 4); s[:, e] = v[1]
    return (c.reshape(128, -1), s)
def pk(c, s):
    return (np.ascontiguousarray(c), mx_ref.live(s))
def emit(q):
    return q[0], q[1]
def packed(v, rng):
    q = [mx_ref.quantize(np.ascontiguousarray(v[r])) for r in range(N)]
    return np.stack([a for a, b in q]), np.stack([mx_ref.plane(b, rng) for a, b in q])
def values_of_codes():
    e, c = np.zeros((128, 128, 4), np.float32), np.zeros((128, 2, 4), np.uint8)
    e[np.arange(128), np.arange(128), 0] = 1
    c[:127, :, 0] = np.arange(256).reshape(2, 128).T[:127]
    return mx_ref.matmul(mx_ref.quantize(e.reshape(128, 512).astype(BF)), (c.reshape(128, 8), np.full((16, 2), 127, np.uint8))).T.reshape(-1).astype(np.float64)
CODE_VALUE, SCALE_VALUE = values_of_codes(), 2.0 ** (np.arange(256) - 127.0)
def decode(q):
    return (CODE_VALUE[q[0]].reshape(16, 8, -1, 4) * SCALE_VALUE[q[1]][:, None, :, None] + 0.0).reshape(128, -1).astype(np.float32)
def f(rng, *shape):
    return mx_ref.flush((rng.standard_normal(shape, dtype=np.float32) * np.exp2(rng.integers(-2, 3, shape[:-1] + (1,)))).astype(BF))
def wide(rng, *shape, cols=0):
    v = rng.standard_normal(shape, dtype=np.float32) * np.exp2(rng.integers(-12, 13, shape)).astype(np.float32)
    if cols: v *= np.repeat(np.exp2(rng.integers(-cols, cols + 1, shape[:-2] + (1, shape[-1] // 4))) * (rng.random(shape[:-2] + (1, shape[-1] // 4)) > 0.0625), 4, axis=-1).astype(np.float32)
    return mx_ref.flush(v.astype(BF))
C, V, B, R = 384, 12, 32, 3
def big(v):
    v = v.astype(np.float32)
    v[np.abs(v) < np.float32(2.0 ** -16)] = 0
    return v.astype(BF)
def numbers_of(rng):
    return {"x": big(f(rng, N, 128, 4 * C)), "u": np.array(f(rng, N, 128, 512)), "v": np.array(f(rng, N, 128, 512))}
def weights(rng, still=[]):
    w = big(f(rng, N, 128, 2048)).reshape(N, 8, 16, 4, 8, 16, 4)
    for i in still:
        w[:, :, i] = 0
        w[:, :, :, :, :, i] = 0
    c, p = packed(w.reshape(N, 128, 2048), rng)
    return {"wc": c, "ws": p}
def yards(h, p):
    return {"hg": np.stack([gtable(h[r].reshape(8, 3 * B)) for r in range(N)]), "dg": np.stack([gtable(p[r]) for r in range(N)])}
def heights(rng):
    c = np.sort(rng.integers(0, V + 1, (N, 8, 2, B)), axis=2)
    return np.concatenate([c[:, :, :1], c[:, :, 1:] - c[:, :, :1], V - c[:, :, 1:]], axis=2)
def deals(rng):
    return np.argsort(rng.random((N, 8, C)), axis=2)
def signs(rng):
    return np.stack([rng.permutation(8) % 2 * 2.0 - 1.0 for r in range(N)])
def setup_inputs(rng):
    return {**numbers_of(rng), **weights(rng), **yards(heights(rng), deals(rng))}
def setup_inputs_ties(rng):
    d = numbers_of(rng)
    e = rng.permutation(N)
    x = d["x"].reshape(N, 8, 16, C, 4)
    for r in range(N):
        k = np.zeros(C, int) if r == e[0] else rng.permutation(C) % 3
        a = x[r][:, :8, :3].copy()
        a[:, :, 2] = 0
        x[r][:, :8] = a[:, :, k]
    x[e[1]] = 0
    u = d["u"].reshape(N, 8, 16, 8, 16, 4)
    k = u.copy()
    u[:, :, :, :, 0] = 0
    for g in range(8): u[:, g, :8, g, 0] = k[:, g, :8, g, 0]
    return {"x": x.reshape(N, 128, 4 * C), "u": u.reshape(N, 128, 512), "v": d["v"], **weights(rng, range(8)), **yards(heights(rng), deals(rng))}
def setup_inputs_near(rng):
    d = numbers_of(rng)
    x = d["x"].astype(np.float32).reshape(N, 8, 16, C, 4)
    u = d["u"].reshape(N, 128, 128, 4)
    x[:, :, 0] = 0
    u[:, :, ::16] = 0
    o, c = rng.permutation(N) % 4, signs(rng)
    for r in range(N):
        t = (V - 1 - (np.arange(V) + rng.integers(0, V, (8, B, 1))) % V).reshape(8, C)
        s = t // 2
        size = 1.0 if o[r] < 2 else 2.0 ** -4
        if o[r] < 2:
            x[r, :, 0, :, 0] = c[r][:, None]
            for i in rng.permutation(8)[:4]: x[r, i, 0, rng.integers(C), 0] *= np.float32(2.0 ** 30)
        if o[r] == 3:
            x[r, :, 1:8] = 0
            x[r, :, 0, :, 0] = (8 + t % 2) * 2.0 ** -30
        x[r, :, 8] = ((s[:, :, None] >> np.arange(4)) & 1) * np.exp2(np.arange(4) - 23.0) * size
        x[r, :, 9:] = rng.integers(4, 8, (8, 7, C, 4)) * 2.0 ** -20 * size
        k = 1.0 if o[r] == 0 else 2.0 ** -30
        for h in range(0, 128, 16):
            u[r, h, h, 0] = k
            u[r, h + 8, h] = k
    return {"x": x.reshape(N, 128, 4 * C).astype(BF), "u": u.reshape(N, 128, 512), "v": d["v"], **weights(rng, [0, 8, 9, 10, 11, 12, 13, 14, 15]), **yards(heights(rng), deals(rng))}
def setup_inputs_stacks(rng):
    d = numbers_of(rng)
    x = d["x"].reshape(N, 8, 16, C, 4)
    u = d["u"].reshape(N, 128, 128, 4)
    h, s = np.zeros((N, 8, 3, B), int), rng.integers(4, 8, (N, 8, B, V))
    for r in range(N):
        for g in range(8):
            c = rng.permutation(B) % 6
            for i in range(B):
                a, l, o = rng.permutation(3)
                m = int(rng.integers(1, V - 2))
                w = np.zeros(3, int)
                w[[a, l, o]] = [(V, 0, 0), (V, 0, 0), (1, V - 1, 0), (V - 2, 0, 2), (V - 2, 1, 1), (2, m, V - 2 - m)][c[i]]
                h[r, g, :, i] = w
                b = [0, w[0], w[0] + w[1]]
                k = s[r, g, i]
                k[b[a] + (V - 1 if c[i] == 1 else 0)] = 1
                if c[i] == 4: k[b[l]] = k[b[o]]
                if c[i] == 5: k[b[o] + rng.integers(w[o])] = 2
    s[rng.permutation(N) < N // 2] -= 12
    x[:, :, 0] = 0
    x[:, :, 0, :, 0] = s.reshape(N, 8, C).astype(np.float32).astype(BF)
    u[:, :, ::16] = 0
    for j in range(0, 128, 16): u[:, j, j, 0] = 1
    p, e = deals(rng), rng.permutation(N)
    p[e[0]] = np.arange(C)
    p[e[1]] = np.arange(C)[::-1]
    return {"x": x.reshape(N, 128, 4 * C), "u": u.reshape(N, 128, 512), "v": d["v"], **weights(rng, [0]), **yards(h, p)}
def setup_inputs_huge(rng):
    d = numbers_of(rng)
    x = 2.0 ** 30 * (0.8 + 0.2 * rng.random((N, 128, C, 4)))
    c = np.stack([rng.permutation(C) % 2 * 2.0 - 1.0 for r in range(N)])
    c[rng.permutation(N) < N // 2] = 1
    x *= c[:, None, :, None]
    u = d["u"].reshape(N, 128, 128, 4)
    a = 2.0 ** 30 * (1 - 0.1 * rng.random((N, 128, 8, 4))) * signs(rng)[:, None, :, None]
    u[:, :, ::16] = a.astype(np.float32).astype(BF)
    w = np.zeros((N, 128, 4, 128, 4), np.float32)
    i = np.arange(128)
    for b in range(4): w[:, i, b, i, b] = -1
    wc, ws = packed(w.reshape(N, 128, 2048).astype(BF), rng)
    return {"x": x.astype(np.float32).reshape(N, 128, 4 * C).astype(BF), "u": u.reshape(N, 128, 512), "v": d["v"], "wc": wc, "ws": ws, **yards(heights(rng), deals(rng))}
def setup_inputs_spread(rng):
    d = setup_inputs(rng)
    d["x"] = big(wide(rng, N, 128, 4 * C, cols=6))
    return d
def check_inputs(d):
    b = []
    for k in ("x", "u", "v"):
        a = np.abs(d[k].astype(np.float32))
        if not (np.isfinite(a).all() and ((a == 0) | (a >= 2.0 ** -30) & (a <= 2.0 ** 30)).all()): b.append("a value of " + k)
    if ((d["wc"] & 0x7F) == 0x7F).any(): b.append("a code of wc that is no number")
    none, least, most = [emit(mx_ref.quantize(np.full((128, 16), k, np.float32).astype(BF)))[1][0, 0] for k in (0.0, 2.0 ** -30, 2.0 ** 30)]
    for r in range(N):
        s = mx_ref.live(d["ws"][r])
        if ((s != none) & ((s < least) | (s > most))).any(): b.append("a scale of ws")
        h = gentries(d["hg"][r]).reshape(8, 3, B)
        if (h < 0).any() or (h > V).any() or (np.sum(h, axis=1) != V).any(): b.append("the heights hg")
        if (np.sort(gentries(d["dg"][r]), axis=1) != np.arange(C)).any(): b.append("dg: no permutation")
    return b
def reference(x, u, v, wc, ws, hg, dg):
    qu = [mx_ref.quantize(u[r]) for r in range(N)]
    lay = [pk(wc[r], ws[r]) for r in range(N)]
    now = [x[r] for r in range(N)]
    high = [gentries(hg[r]).reshape(8, 3, B).transpose(0, 2, 1) for r in range(N)]
    place, three, start = np.arange(V), np.arange(3), V * np.arange(B)[:, None]
    for t in range(R):
        sent, moved = [], []
        for r in range(N):
            s = (mx_ref.matmul(qu[r], mx_ref.quantize(now[r]))[::16] + np.float32(0.0)).reshape(8, B, V)
            h = high[r]
            end = np.stack([h[:, :, 0], h[:, :, 0] + h[:, :, 1], np.full((8, B), V)], axis=2)
            stack = (place >= end[:, :, :1]).astype(int) + (place >= end[:, :, 1:2])
            k = np.argmin(s, axis=2)[:, :, None]
            a = np.take_along_axis(stack, k, axis=2)
            low = np.stack([np.min(np.where(stack == i, s, np.float32(np.inf)), axis=2) for i in range(3)], axis=2)
            low[three == a] = -np.inf
            l = np.argmax(low, axis=2)[:, :, None]
            up = (stack == a) & (place > k)
            m = np.where(up & (np.take_along_axis(h, l, axis=2) > 0), np.take_along_axis(end, l, axis=2) - 1, place)
            key = np.where(up, 4 * V * l + 2 * V - place, 4 * V * stack + place)
            key = np.where(place == k, 4 * V * a + 3 * V, key)
            o = np.argsort(key, axis=2)
            high[r] = h + np.sum(up, axis=2)[:, :, None] * ((three == l).astype(int) - (three == a).astype(int))
            moved.append(((start + o).reshape(8, C), (start + np.take_along_axis(m, o, axis=2)).reshape(8, C), (o == k).reshape(8, C)))
            sent.append(mx_ref.quantize(gcols(now[r], (start + k).reshape(8, B))))
        came = decode(join(*sent)).astype(BF)
        for r in range(N):
            c = np.ascontiguousarray(cut(came, (r - 1) % N, 4 * B))
            q = mx_ref.quantize(c)
            new = tile([mx_ref.matmul(pick(lay[r], np.arange(128 * b, 128 * b + 128)), q) * np.float32(0.015625) + c[:, b::4].astype(np.float32) for b in range(4)])
            e, m, arrived = moved[r]
            z = ((gcols(now[r], e).astype(np.float32) + gcols(now[r], m).astype(np.float32)) * np.float32(0.5)).astype(BF)
            yard = np.where(arrived, C + np.arange(C) // V, np.arange(C))
            now[r] = gcols(np.concatenate([z, new], axis=1), np.take_along_axis(yard, gentries(dg[r]), axis=1))
    y, oh = np.zeros((N, 128, C), np.float32), np.zeros((N, 8, 3 * B), np.float32)
    oc, osc = np.zeros((N, 128, 4 * C), np.uint8), np.zeros((N, 16, C), np.uint8)
    for r in range(N):
        q = mx_ref.quantize(now[r])
        y[r] = mx_ref.matmul(mx_ref.quantize(v[r]), q)
        oh[r] = high[r].transpose(0, 2, 1).reshape(8, 3 * B)
        oc[r], osc[r] = emit(q)
    return {"y": y, "oh": oh, "oc": oc, "osc": osc}

@@ -1,0 +1,495 @@
+from concourse.bass import DstId, RemoteDMATransfer
+from concourse.mybir import dt, AluOpType, AxisListType, ActivationFunctionType
+
+C, V, B, R = 384, 12, 32, 3
+HC = C // 2
+BIG = 2.0 ** 98
+UP = 2.0 ** 19
+Q4, U8 = "float8_e4m3fn_x4", "uint8"
+
+SCRATCH = {"ps": ("psum", [128, 4096], "float32")}
+
+
+def _buf(name, n, dtype):
+    SCRATCH[name] = ("sbuf", [128, n], dtype)
+
+
+for _r in range(R + 1):
+    _buf("X%d" % _r, 4 * C, "bfloat16")
+    _buf("QX%d" % _r, C, Q4)
+    _buf("SX%d" % _r, C, U8)
+for _r in range(R):
+    _buf("QA%d" % _r, 128, Q4)
+    _buf("SA%d" % _r, 128, U8)
+    _buf("LQ%d" % _r, 160, Q4)
+    _buf("LS%d" % _r, 256, U8)
+for _n, _w, _d in [
+        ("XH", 4 * C, "bfloat16"),
+        ("T1", 4 * C, "bfloat16"), ("U", 512, "bfloat16"), ("Vt", 512, "bfloat16"), ("QU", 128, Q4), ("SU", 128, U8),
+        ("QUR", 128, Q4), ("SUR", 128, U8), ("QV", 128, Q4), ("SV", 128, U8), ("WQ", 512, Q4), ("WS", 512, U8),
+        ("F0", 520, "bfloat16"), ("F1", 520, "bfloat16"), ("QE", 512, Q4), ("SE", 512, U8), ("AG", 640, "bfloat16"),
+        ("QG", 128, Q4), ("SG", 128, U8), ("H", 128, "bfloat16"),
+        ("HG", 8, "int32"), ("DG", 24, "int32"), ("ci", 16, "int32"), ("uo", 8, "uint16"), ("cf", 512, "float32"),
+        ("D16", 16, "float32"), ("DS", HC, "float32"), ("ql", 24, "uint16"),
+        ("j4", C, "float32"), ("DINV", C, "float32"), ("TR", 64, "float32"), ("MK", C, "float32"), ("SS", C, "float32"),
+        ("PM", C, "float32"), ("PS", C, "float32"), ("w", 2048, "float32"), ("wi", 256, "int32"), ("wu", 256, "uint16"),
+        ("TH", 32, "float32"), ("TT", 32, "float32"), ("Y", C, "float32")]:
+    _buf(_n, _w, _d)
+
+NDMA = 40
+SEMAPHORES = ["qv", "qs", "qt", "qg"] + ["d%d" % i for i in range(NDMA)] + \
+             ["arr%d" % r for r in range(R)] + ["out%d" % r for r in range(R)]
+
+Op, Act = AluOpType, ActivationFunctionType
+
+
+def rank_program(g, core, T, topo):
+    rank = T.rank_of(core)
+    if rank is None:
+        return
+    nxt = T.cores[(rank + 1) % len(T.cores)]
+    ops = []
+    eng = {"v": g.vector, "s": g.scalar, "t": g.tensor, "g": g, "y": g.sync}
+
+    def vw(name, a, b, s=1):
+        m = 0
+        for c in range(a, b, s):
+            m |= 1 << c
+        ap = T[name][:, a:b] if s == 1 else T[name][:, a:b:s]
+        return (ap, name, m)
+
+    def ind(win, off, words=False):
+        ap = win[0].bitcast(dt.uint32) if words else win[0]
+        return (ap.indirect(off[0]), win[1], win[2], off)
+
+    def acc(views):
+        out = []
+        for x in views:
+            if isinstance(x, tuple):
+                out.append((x[1], x[2]))
+                if len(x) == 4:
+                    out.append((x[3][1], x[3][2]))
+        return out
+
+    def ap(x):
+        return x[0] if isinstance(x, tuple) else x
+
+    def add(q, fn, reads, writes, kind="c", sem=None, cnt=0):
+        rd = acc(reads) + [(x[3][1], x[3][2]) for x in writes if len(x) == 4]
+        ops.append({"q": q, "fn": fn, "r": rd, "w": [(x[1], x[2]) for x in writes], "kind": kind, "sem": sem, "cnt": cnt})
+
+    def tt(out, a, b, op):
+        add("v", lambda: g.vector.tensor_tensor(out[0], a[0], b[0], op), [a, b], [out])
+
+    def ts(out, a, s1, op0, s2=None, op1=None):
+        if op1 is None:
+            add("v", lambda: g.vector.tensor_scalar(out[0], a[0], ap(s1), None, op0), [a, s1], [out])
+        else:
+            add("v", lambda: g.vector.tensor_scalar(out[0], a[0], ap(s1), ap(s2), op0, op1), [a, s1, s2], [out])
+
+    def cp(out, a):
+        add("v", lambda: g.vector.tensor_copy(out[0], a[0]), [a], [out])
+
+    def scan(out, d0, d1, init, op0, op1):
+        add("v", lambda: g.vector.tensor_tensor_scan(out[0], d0[0], d1[0], init, op0, op1), [d0, d1], [out])
+
+    def ms(out, val):
+        add("v", lambda: g.vector.memset(out[0], val), [], [out])
+
+    def quant(q, s, x):
+        add("v", lambda: g.vector.quantize_mx(q[0], s[0], x[0]), [x], [q, s])
+
+    def turn(out, a):
+        add("v", lambda: g.vector.transpose(out[0], a[0]), [a], [out])
+
+    def least(out, a):
+        add("v", lambda: g.vector.tensor_reduce(out[0], a[0], AxisListType.X, Op.min), [a], [out])
+
+    def act(out, a, func=Act.Identity, scale=1.0, bias=None):
+        if func == Act.Copy:
+            add("s", lambda: g.scalar.activation(out[0], a[0], func), [a], [out])
+        elif bias is None:
+            add("s", lambda: g.scalar.activation(out[0], a[0], func, scale=ap(scale)), [a, scale], [out])
+        else:
+            add("s", lambda: g.scalar.activation(out[0], a[0], func, bias=ap(bias), scale=ap(scale)), [a, scale, bias], [out])
+
+    def mm(bank, n, wq, ws, xq, xs, start=True, stop=True):
+        out = vw("ps", 512 * bank, 512 * bank + n)
+        add("t", lambda: g.tensor.matmul_mx(out[0], wq[0], ws[0], xq[0], xs[0], start, stop), [wq, ws, xq, xs], [out])
+
+    def iota(out, pattern, base, cm=0, small=True):
+        if small:
+            add("g", lambda: g.iota(out[0], pattern, base, cm, allow_small_or_imprecise_dtypes=True), [], [out])
+        else:
+            add("g", lambda: g.iota(out[0], pattern, base, cm), [], [out])
+
+    ndma = [0]
+
+    def dma(q, out, in_, reads, writes):
+        sem = T.sem["d%d" % ndma[0]]
+        ndma[0] += 1
+        add(q, lambda: eng[q].dma_start(out, in_), reads, writes, "d", sem, 16)
+
+    top = {"w": 0, "wi": 0, "wu": 0, "cf": 0}
+
+    def al(n, name="w"):
+        a = top[name]
+        top[name] = a + n + n % 2
+        return lambda lo=0, hi=n, s=1: vw(name, a + lo, a + hi, s)
+
+    def whole(name):
+        return vw(name, 0, SCRATCH[name][1][1])
+
+    def bytes_of(x):
+        return x[0].bitcast(dt.uint8)
+
+    dma("s", T.HG[:, 0:6], T.hg[:], [], [whole("HG")])
+    dma("s", T.DG[:], T.dg[:], [], [whole("DG")])
+    dma("y", T.U[:], T.u[:], [], [whole("U")])
+    for h in range(2):
+        dma("y", T.X0[:, 4 * HC * h:4 * HC * (h + 1)], T.x[:, 4 * HC * h:4 * HC * (h + 1)], [], [vw("X0", 4 * HC * h, 4 * HC * (h + 1))])
+
+    pint, uoi, pti = vw("ci", 0, 1), vw("ci", 8, 16), lambda k: vw("ci", k, k + 1)
+    yc, i4, mq, keep4, keep, m64, m64i = al(26, "cf"), al(32, "cf"), al(32, "cf"), al(32, "cf"), al(96, "cf"), al(64, "cf"), al(64)
+    pf, d0k, rst, ones, d0p, sc = al(4, "cf"), al(28, "cf"), al(36, "cf"), al(2, "cf"), al(72, "cf"), al(1, "cf")
+    ycol = yc(1, 13)
+    tk, pkin, da, db = al(28), al(72), al(16), al(16)
+    EM, E0 = [al(8) for r in range(R + 1)], [al(4) for r in range(R + 1)]
+    atile, gtile = vw("AG", 0, 512), vw("AG", 128, 640)
+
+    def fill(out, n, val):
+        act(out, vw("F0", 0, n), scale=0.0, bias=float(val))
+
+    ms(whole("F0"), 64.0)
+    iota(pint, [[0, 1]], 0, 1, False)
+    iota(uoi, [[16, 8]], 0, 0, False)
+    iota(yc(), [[1, 26]], -1)
+    add("g", lambda: g.affine_select(T.F1[:], T.F0[:], [[-1, 520]], Op.is_equal, 0.0, 3, 4), [whole("F0")], [whole("F1")])
+    iota(whole("j4"), [[4, C]], 0)
+    iota(m64i(), [[1, 16], [0, 4]], 0)
+    iota(i4(), [[0, 8], [1, 4]], 0)
+    iota(whole("TH"), [[0, 32]], 0)
+    fill(pkin(), 72, 0)
+    fill(keep(), 96, 1)
+    fill(d0k(), 28, -1)
+    fill(tk(), 28, 5000)
+    fill(rst(), 36, -2.0 * BIG)
+    fill(d0p(), 72, 1)
+    fill(keep4(), 32, 1)
+    fill(keep(0, 96, 16), 6, 0)
+    fill(d0k(0, 28, 14), 2, 5000)
+    fill(d0k(12, 28, 14), 2, V)
+    fill(rst(0, 36, 12), 3, 2.0 * BIG)
+    for h in range(2):
+        fill(d0p(36 * h + 1, 36 * h + 4), 3, 16)
+    fill(d0p(0, 72, 36), 2, 0)
+    fill(keep4(0, 32, 4), 8, 0)
+    fill(ones(), 2, 1)
+    for r in range(R):
+        fill(EM[r](4, 8), 4, V)
+    ms(gtile, 0.0)
+    ts(pti(1), pint, 15, Op.bitwise_and)
+    ts(pti(2), pint, 2, Op.logical_shift_right, 3, Op.bitwise_and)
+    ts(pti(3), pint, 3, Op.bitwise_and)
+    ts(pti(4), pint, 16, Op.bitwise_and)
+    cp(whole("uo"), uoi)
+    cp(pf(), vw("ci", 1, 5))
+    quant(vw("LQ0", 0, 128), vw("LS0", 0, 128), gtile)
+    dma("y", bytes_of(whole("WQ")), T.wc[:], [], [whole("WQ")])
+    dma("y", T.WS[:], T.ws[:], [], [whole("WS")])
+    for r in range(1, R):
+        dma("y", bytes_of(vw("LQ%d" % r, 0, 128)), bytes_of(vw("LQ0", 0, 128)), [vw("LQ0", 0, 128)], [vw("LQ%d" % r, 0, 128)])
+        dma("y", vw("LS%d" % r, 0, 128)[0], vw("LS0", 0, 128)[0], [vw("LS0", 0, 128)], [vw("LS%d" % r, 0, 128)])
+    dma("y", T.Vt[:], T.v[:], [], [whole("Vt")])
+    ts(da(), yc(1, 17), pf(0, 1), Op.not_equal)
+    ts(db(), yc(0, 16), pf(0, 1), Op.is_equal, UP - 1.0, Op.mult)
+    ts(whole("ql"), yc(0, 24), 0.0, Op.mult, pf(0, 1), Op.add)
+    ts(sc(), pf(0, 1), 15.0, Op.is_equal, 1.0 / UP, Op.max)
+    tt(whole("D16"), da(), db(), Op.add)
+    for h in range(2):
+        ts(d0k(14 * h + 13, 14 * h + 14), pf(0, 1), float(V), Op.mult, float(HC * h - 1), Op.add)
+    act(whole("DS"), ind(whole("D16"), vw("ql", 0, 12)))
+    for b in range(4):
+        quant(vw("QE", 128 * b, 128 * b + 128), vw("SE", 128 * b, 128 * b + 128), vw("F1", 3 - b, 515 - b))
+    for k in range(2):
+        cp(E0[0](k, 4, 2), vw("HG", 0, 2))
+        tt(EM[0](k, 4, 2), vw("HG", 0, 2), vw("HG", 2, 4), Op.add)
+
+    pen = al(72)
+
+    def pens(r):
+        b0, b2, uu, ub, ba, bb, ab, h1, h2, pr = al(2), al(2), al(2), al(2), al(2), al(2), al(24), al(2), al(2), al(2)
+        e0, e1 = E0[r](0, 4, 2), EM[r](0, 4, 2)
+        e0h = lambda h: E0[r](2 * h, 2 * h + 1)
+        act(uu(), e1, scale=-1.0, bias=1.0)
+        act(ub(), e1, scale=-BIG / 2, bias=BIG / 2)
+        act(b0(), e0, scale=-BIG, bias=BIG)
+        act(b2(), e1, scale=BIG)
+        act(h2(), e1, scale=-1.0, bias=float(V))
+        for h in range(2):
+            act(ba(h, h + 1), e0h(h), scale=-1.0, bias=uu(h, h + 1))
+            act(h1(h, h + 1), e0h(h), scale=-1.0, bias=EM[r](2 * h, 2 * h + 1))
+        for h in range(2):
+            act(bb(h, h + 1), e0h(h), scale=BIG / 2, bias=ub(h, h + 1))
+        for h in range(2):
+            act(ab(12 * h, 12 * h + 12), ycol, Act.Abs, 2.0, ba(h, h + 1))
+            act(pr(h, h + 1), e0h(h), scale=h1(h, h + 1))
+        for h in range(2):
+            act(pen(h, 24, 2), ycol, Act.Relu, BIG, b0(h, h + 1))
+            act(pen(48 + h, 72, 2), ycol, Act.Relu, -BIG, b2(h, h + 1))
+        for h in range(2):
+            act(pen(24 + h, 48, 2), ab(12 * h, 12 * h + 12), Act.Relu, BIG / 2, bb(h, h + 1))
+            act(pkin(36 * h, 36 * h + 1), pr(h, h + 1), Act.Sign, h2(h, h + 1))
+
+    df, t24, i24, yy, g24, t25 = al(24), al(24), al(24), al(48), al(24), al(24)
+    ii = al(24, "wi")
+    du, itu = al(24, "wu"), al(24, "wu")
+    later = [lambda: cp(df(), whole("DG")),
+             lambda: cp(ii(), t24()),
+             lambda: ts(g24(), ii(), 16.0, Op.is_ge, 16.0, Op.mult),
+             lambda: ts(i24(), ii(), -float(V), Op.mult),
+             lambda: tt(t25(), g24(), ii(), Op.add),
+             lambda: tt(yy(0, 24), df(), i24(), Op.add),
+             lambda: ts(itu(), t25(), pf(3, 4), Op.add),
+             lambda: tt(yy(24, 48), df(), i24(), Op.add),
+             lambda: ts(mq(), i4(), pf(1, 2), Op.is_equal),
+             lambda: quant(whole("QV"), whole("SV"), whole("Vt"))]
+
+    def meanwhile(n=1):
+        for k in range(min(n, len(later))):
+            later.pop(0)()
+
+    cp(du(), whole("DG"))
+    ts(t24(), whole("DG"), -5.5, Op.add, 1.0 / V, Op.mult)
+    cp(ind(whole("DINV"), du()), whole("j4"))
+    quant(whole("QU"), whole("SU"), whole("U"))
+    ts(m64(), m64i(), pf(0, 1), Op.is_equal)
+    qur = whole("QUR")
+    add("v", lambda: g.vector.tensor_copy(qur[0].bitcast(dt.uint32), ind(whole("QU"), whole("uo"), True)[0]),
+        [whole("QU"), whole("uo")], [qur])
+    pens(0)
+    act(whole("SUR"), ind(whole("SU"), whole("uo")), Act.Copy)
+
+    mn, lp, lw, fa, t8, t4, ela = al(2), al(72), al(72), al(12), al(8), al(4), al(4)
+    m01, c10, nb, dd, dn, pko = al(2), al(2), al(2), al(4), al(4), al(72)
+    tko = al(28)
+    pk, ff = al(24, "wi"), al(96, "wi")
+    nm1, uz, gg, gd, t1, o0, isb, t3, un, em = al(24), al(72), al(72), al(24), al(24), al(24), al(24), al(24), al(24), al(48)
+    t5, t6, phm, phs = al(24), al(24), al(32), al(32)
+    eng8 = topo.engines(core, nxt)
+    half = len(eng8) // 2
+    masks = [sum(1 << e for e in eng8[:half]), sum(1 << e for e in eng8[half:])]
+    rid, pid = topo.addr(nxt)[:2]
+
+    def halves(r, wq, ws, bank):
+        for h in range(2):
+            qx, sx = vw("QX%d" % r, HC * h, HC * h + HC), vw("SX%d" % r, HC * h, HC * h + HC)
+            quant(qx, sx, vw("X%d" % r, 4 * HC * h, 4 * HC * (h + 1)))
+            mm(bank + h, HC, whole(wq), whole(ws), qx, sx)
+
+    plane = lambda t: vw("XH", C * t, C * t + C)
+
+    for r in range(R):
+        X, XN = "X%d" % r, "X%d" % (r + 1)
+        ku, lu, lh, ph = al(2, "wu"), al(48, "wu"), al(2, "wu"), al(8, "wu")
+        halves(r, "QUR", "SUR", 0)
+        for t in range(4):
+            act(plane(t), vw(X, t, 4 * C, 4), scale=0.5)
+        meanwhile(2)
+        for h in range(2):
+            for k in range(3):
+                a = 128 * k + 64 * h
+                tt(vw("MK", a, a + 64), vw("ps", 512 * h + k, 512 * h + HC, 3), m64(), Op.mult)
+        meanwhile()
+        for k in range(4):
+            scan(vw("SS", 96 * k, 96 * k + 96), keep(), vw("MK", k, C, 4), 0.0, Op.mult, Op.add)
+        meanwhile()
+        for h in range(2):
+            least(mn(h, h + 1), vw("SS", 16 * h + 15, C, 32))
+        tt(lp(0, 24), vw("SS", 15, C, 16), pen(0, 24), Op.add)
+        for h in range(2):
+            ts(tk(14 * h, 14 * h + 12), vw("SS", 16 * h + 15, C, 32), mn(h, h + 1), Op.is_gt, 1000.0, Op.mult)
+        tt(lp(24, 48), vw("SS", 15, C, 16), pen(24, 48), Op.add)
+        scan(tko(), d0k(), tk(), 0.0, Op.add, Op.min)
+        tt(lp(48, 72), vw("SS", 15, C, 16), pen(48, 72), Op.add)
+        cp(ku(), tko(13, 28, 14))
+        for t in range(4):
+            act(vw("AG", t, 128, 4), ind(plane(t), ku()), scale=2.0)
+        for h in range(2):
+            scan(lw(36 * h, 36 * h + 36), rst(), lp(h, 72, 2), 0.0, Op.max, Op.min)
+        k1 = lambda h: tko(14 * h + 12, 14 * h + 13)
+        k12 = tko(12, 28, 14)
+        low = lambda s: lw(11 + 12 * s, 72, 36)
+        tt(fa(1, 4, 2), k12, E0[r](0, 4, 2), Op.is_gt)
+        tt(m01(), low(0), low(1), Op.max)
+        tt(c10(), low(1), low(0), Op.is_gt)
+        tt(fa(5, 8, 2), k12, EM[r](0, 4, 2), Op.is_gt)
+        tt(fa(4, 8, 2), low(2), m01(), Op.is_gt)
+        tt(fa(0, 4, 2), c10(), fa(1, 4, 2), Op.is_ge)
+        qa, sa = whole("QA%d" % r), whole("SA%d" % r)
+        quant(qa, sa, atile)
+        lq, ls = vw("LQ%d" % r, 128, 160), vw("LS%d" % r, 128, 256)
+
+        def send(r=r, qa32=vw("QA%d" % r, 0, B), sa=sa, lq=lq, ls=ls):
+            to = [DstId(rid=rid, pnc=pid)]
+            arr = T.sem["arr%d" % r]
+            return g.remote_dma_fused(
+                [RemoteDMATransfer(dst_ids=to, dma_engine_mask=masks[0], remote_sem=arr, src=bytes_of(qa32), dst=bytes_of(lq)),
+                 RemoteDMATransfer(dst_ids=to, dma_engine_mask=masks[1], remote_sem=arr, src=sa[0], dst=ls[0])],
+                local_sem=T.sem["out%d" % r])
+        add("g", send, [qa, sa], [], "r", T.sem["out%d" % r], 2 * half)
+        add("x", None, [], [lq, ls], "x", T.sem["arr%d" % r], 2 * half)
+        lqv, lsv = vw("LQ%d" % r, 32, 160), vw("LS%d" % r, 32, 160)
+        for b in range(8):
+            e = 128 * (b % 4)
+            mm(b, 128, vw("QE", e, e + 128), vw("SE", e, e + 128), lqv, lsv, True, b < 4)
+        tt(t8(), fa(0, 8), EM[r](), Op.mult)
+        tt(fa(8, 12), fa(0, 4), fa(4, 8), Op.max)
+        tt(t4(), t8(0, 4), t8(4, 8), Op.max)
+        tt(dd(), fa(5, 12, 2), fa(4, 12, 2), Op.subtract)
+        tt(ela(), t4(), E0[r](), Op.max)
+        meanwhile()
+        tt(pkin(1, 72, 36), ela(1, 4, 2), k12, Op.subtract)
+        meanwhile()
+        nn = lambda h: pkin(36 * h + 1, 36 * h + 2)
+        for h in range(2):
+            ts(nb(h, h + 1), ela(2 * h, 2 * h + 1), k1(h), Op.is_ge, nn(h), Op.mult)
+        for h in range(2):
+            ts(pkin(36 * h + 2, 36 * h + 4), ela(2 * h, 2 * h + 2), nb(h, h + 1), Op.subtract)
+        ts(lh(0, 1), pkin(3, 4), d0k(13, 14), Op.add)
+        for h in range(2):
+            act(dn(h, 4, 2), dd(h, 4, 2), scale=nn(h))
+        for h in range(2):
+            act(EM[r + 1](2 * h, 2 * h + 2), ones(), scale=dn(h, h + 1), bias=EM[r](2 * h, 2 * h + 1))
+            act(E0[r + 1](2 * h, 2 * h + 2), ones(), scale=dn(2 + h, 3 + h), bias=E0[r](2 * h, 2 * h + 1))
+        scan(pko(), d0p(), pkin(), 0.0, Op.mult, Op.add)
+        ts(lh(1, 2), pkin(39, 40), d0k(27, 28), Op.add)
+        for h in range(2):
+            turn(vw("TR", 32 * h, 32 * h + 32), pko(36 * h + 4, 36 * h + 36))
+        meanwhile()
+        act(vw("PM", HC, C), ind(whole("TR"), itu(12, 24)))
+        cp(vw("PM", 0, HC), ind(whole("TR"), itu(0, 12)))
+        meanwhile()
+        for h in range(2):
+            scan(vw("PS", HC * h, HC * h + HC), whole("DS"), vw("PM", HC * h, HC * h + HC), 0.0, Op.mult, Op.add)
+        if r + 1 < R:
+            pens(r + 1)
+        else:
+            act(vw("TH", 0, 2), E0[R](0, 4, 2))
+            act(vw("TH", 4, 6), EM[R](0, 4, 2), scale=-1.0, bias=float(V))
+            for h in range(2):
+                act(vw("TH", 2 + h, 3 + h), E0[R](2 * h, 2 * h + 1), scale=-1.0, bias=EM[R](2 * h, 2 * h + 1))
+        meanwhile()
+        ts(pk(), vw("PS", 15, C, 16), sc(), Op.mult, 2.0 ** 23, Op.add)
+        tt(phm(), ind(whole("DINV"), lh()), mq(), Op.mult)
+        fn_, fne = ff(48, 72), ff(72, 96)
+        ts(ff(0, 24), pk(), 15, Op.bitwise_and)
+        ts(ff(24, 48), pk(), 4, Op.logical_shift_right, 15, Op.bitwise_and)
+        ts(fn_, pk(), 8, Op.logical_shift_right, 15, Op.bitwise_and)
+        tt(uz(0, 48), yy(), ff(0, 48), Op.subtract)
+        ts(nm1(), fn_, -1.0, Op.add)
+        ts(gg(0, 48), uz(0, 48), 0.0, Op.is_ge)
+        tt(uz(48, 72), nm1(), uz(24, 48), Op.subtract)
+        tt(gd(), gg(0, 24), gg(24, 48), Op.subtract)
+        ts(gg(48, 72), uz(48, 72), 0.0, Op.is_ge)
+        tt(t3(), uz(48, 72), uz(0, 24), Op.subtract)
+        tt(isb(), gg(24, 48), gg(48, 72), Op.mult)
+        tt(t1(), gd(), fn_, Op.mult)
+        tt(t5(), t3(), isb(), Op.mult)
+        tt(o0(), t1(), df(), Op.add)
+        ts(fne, pk(), 12, Op.logical_shift_right, 1, Op.bitwise_and)
+        tt(em(0, 24), o0(), t5(), Op.add)
+        tt(un(), uz(0, 24), fne, Op.mult)
+        cp(lu(0, 24), em(0, 24))
+        tt(t6(), un(), isb(), Op.mult)
+        scan(phs(), keep4(), phm(), 0.0, Op.mult, Op.add)
+        tt(em(24, 48), em(0, 24), t6(), Op.add)
+        ts(ph(), phs(3, 32, 4), pf(2, 3), Op.add)
+        cp(lu(24, 48), em(24, 48))
+        meanwhile(9)
+        if r == R - 1:
+            turn(whole("TT"), whole("TH"))
+            for k in range(8):
+                a, p = k // 2, k % 2
+                dma("y", T.oh[k, :], T.TT[32 * a:32 * a + 6, 16 * p:16 * p + 16], [whole("TT")], [])
+
+        for t in range(4):
+            if t == 2:
+                for b in range(4):
+                    act(vw("AG", 512 + b, 640, 4), vw("ps", 512 * b + 96, 512 * b + 128), scale=2.0 ** -6)
+                quant(whole("QG"), whole("SG"), gtile)
+                for b in range(4):
+                    e = 128 * b
+                    mm(4 + b, 128, vw("WQ", e, e + 128), vw("WS", e, e + 128), whole("QG"), whole("SG"), False, True)
+            for h in range(2):
+                t1v = vw("T1", C * t + HC * h, C * t + HC * h + HC)
+                act(t1v, ind(plane(t), lu(12 * h, 12 * h + 12)))
+                tt(vw(XN, 4 * HC * h + t, 4 * HC * (h + 1), 4), ind(plane(t), lu(24 + 12 * h, 36 + 12 * h)), t1v, Op.add)
+        for b in range(4):
+            act(vw("H", b, 128, 4), vw("ps", 512 * (4 + b) + 96, 512 * (4 + b) + 128), scale=2.0 ** -6)
+        cp(ind(whole(XN), ph()), whole("H"))
+
+    halves(R, "QV", "SV", 2)
+    for h in range(2):
+        qx = vw("QX%d" % R, HC * h, HC * h + HC)
+        dma("y", T.oc[:, 4 * HC * h:4 * HC * (h + 1)], bytes_of(qx), [qx], [])
+    act(vw("Y", 0, HC), vw("ps", 1024, 1024 + HC))
+    dma("s", T.y[:, 0:HC], T.Y[:, 0:HC], [vw("Y", 0, HC)], [])
+    cp(vw("Y", HC, C), vw("ps", 1536, 1536 + HC))
+    dma("s", T.y[:, HC:C], T.Y[:, HC:C], [vw("Y", HC, C)], [])
+    for k in range(4):
+        dma("y", T.osc[4 * k:4 * k + 4, :], T["SX%d" % R][32 * k:32 * k + 4, :], [whole("SX%d" % R)], [])
+
+    qsem = {"v": T.sem.qv, "s": T.sem.qs, "t": T.sem.qt, "g": T.sem.qg}
+    count = {"v": 0, "s": 0, "t": 0, "g": 0}
+    know = {q: {} for q in eng}
+    hist = {}
+
+    def banks(m):
+        return [k for k in range(8) if (m >> (512 * k)) & ((1 << 512) - 1)]
+
+    for i, o in enumerate(ops):
+        q = o["q"]
+        need = set()
+        for name, m, wr in [(n, m, False) for n, m in o["r"]] + [(n, m, True) for n, m in o["w"]]:
+            for j, mj, wj in hist.get(name, []):
+                p = ops[j]
+                if name == "ps" and p["q"] != q:
+                    if set(banks(m)) & set(banks(mj)):
+                        need.add(j)
+                elif (m & mj) and (wr or wj) and not (q == "t" and p["q"] == "t"):
+                    need.add(j)
+        for name, m in o["r"]:
+            hist.setdefault(name, []).append((i, m, False))
+        for name, m in o["w"]:
+            hist.setdefault(name, []).append((i, m, True))
+        if o["kind"] == "c":
+            count[q] += 1
+            o["key"], o["sem"], o["cnt"] = q, qsem[q], count[q]
+        else:
+            o["key"] = i
+        if o["kind"] == "x":
+            o["clock"] = {i: o["cnt"]}
+            continue
+        kn = know[q]
+        for j in sorted(need, reverse=True):
+            p = ops[j]
+            if kn.get(p["key"], 0) < p["cnt"]:
+                eng[q].wait_ge(p["sem"], p["cnt"])
+                for k, c in p["clock"].items():
+                    if kn.get(k, 0) < c:
+                        kn[k] = c
+        ins = o["fn"]()
+        if o["kind"] == "c":
+            ins.then_inc(o["sem"], 1)
+        elif o["kind"] == "d":
+            ins.then_inc(o["sem"], 16)
+        o["clock"] = dict(kn)
+        o["clock"][o["key"]] = o["cnt"]
+    kn = know["g"]
+    for o in reversed(ops):
+        if kn.get(o["key"], 0) < o["cnt"]:
+            g.wait_ge(o["sem"], o["cnt"])
+            for k, c in o["clock"].items():
+                if kn.get(k, 0) < c:
+                    kn[k] = c

@@ -5,6 +5,7 @@ C, V, B, R = 384, 12, 32, 3
 HC = C // 2
 BIG = 2.0 ** 98
 UP = 2.0 ** 19
+WAKE, SLACK, FLIGHT = 0.17, 0.03, 4.3
 Q4, U8 = "float8_e4m3fn_x4", "uint8"
 
 SCRATCH = {"ps": ("psum", [128, 4096], "float32")}
@@ -74,9 +75,27 @@ def rank_program(g, core, T, topo):
     def ap(x):
         return x[0] if isinstance(x, tuple) else x
 
+    def cost(q, kind, reads, writes):
+        if kind != "c":
+            return 0.1
+        o = writes[0]
+        n = bin(o[2]).count("1")
+        if len(o) == 4:
+            return 0.05 + 0.048 * bin(o[3][2]).count("1")
+        if q == "t":
+            return 0.0008 * (n + 16)
+        if q == "g":
+            return 0.15 + 0.002 * n
+        if any(isinstance(x, tuple) and len(x) == 4 for x in reads):
+            return 0.05 + 0.0015 * n
+        if len(writes) == 2:
+            return 0.015 + 0.00105 * n
+        return max(0.064, 0.001 * n)
+
     def add(q, fn, reads, writes, kind="c", sem=None, cnt=0):
         rd = acc(reads) + [(x[3][1], x[3][2]) for x in writes if len(x) == 4]
-        ops.append({"q": q, "fn": fn, "r": rd, "w": [(x[1], x[2]) for x in writes], "kind": kind, "sem": sem, "cnt": cnt})
+        ops.append({"q": q, "fn": fn, "cost": cost(q, kind, reads, writes), "r": rd, "w": [(x[1], x[2]) for x in writes],
+                    "kind": kind, "sem": sem, "cnt": cnt})
 
     def tt(out, a, b, op):
         add("v", lambda: g.vector.tensor_tensor(out[0], a[0], b[0], op), [a, b], [out])
@@ -150,8 +169,8 @@ def rank_program(g, core, T, topo):
         dma("y", T.X0[:, 4 * HC * h:4 * HC * (h + 1)], T.x[:, 4 * HC * h:4 * HC * (h + 1)], [], [vw("X0", 4 * HC * h, 4 * HC * (h + 1))])
 
     pint, uoi, pti = vw("ci", 0, 1), vw("ci", 8, 16), lambda k: vw("ci", k, k + 1)
-    yc, i4, mq, keep4, keep, m64, m64i = al(26, "cf"), al(32, "cf"), al(32, "cf"), al(32, "cf"), al(96, "cf"), al(64, "cf"), al(64)
-    pf, d0k, rst, ones, d0p, sc = al(4, "cf"), al(28, "cf"), al(36, "cf"), al(2, "cf"), al(72, "cf"), al(1, "cf")
+    yc, i4, mq, keep4, keep, m64, m64i = al(26, "cf"), al(32, "cf"), al(32, "cf"), al(32, "cf"), al(48, "cf"), al(64, "cf"), al(64)
+    pf, d0k, rst, ones, d0p, sc = al(4, "cf"), al(28, "cf"), al(72, "cf"), al(2, "cf"), al(72, "cf"), al(1, "cf")
     ycol = yc(1, 13)
     tk, pkin, da, db = al(28), al(72), al(16), al(16)
     EM, E0 = [al(8) for r in range(R + 1)], [al(4) for r in range(R + 1)]
@@ -164,24 +183,24 @@ def rank_program(g, core, T, topo):
     iota(pint, [[0, 1]], 0, 1, False)
     iota(uoi, [[16, 8]], 0, 0, False)
     iota(yc(), [[1, 26]], -1)
-    add("g", lambda: g.affine_select(T.F1[:], T.F0[:], [[-1, 520]], Op.is_equal, 0.0, 3, 4), [whole("F0")], [whole("F1")])
     iota(whole("j4"), [[4, C]], 0)
     iota(m64i(), [[1, 16], [0, 4]], 0)
+    add("g", lambda: g.affine_select(T.F1[:], T.F0[:], [[-1, 520]], Op.is_equal, 0.0, 3, 4), [whole("F0")], [whole("F1")])
     iota(i4(), [[0, 8], [1, 4]], 0)
     iota(whole("TH"), [[0, 32]], 0)
     fill(pkin(), 72, 0)
-    fill(keep(), 96, 1)
+    fill(keep(), 48, 1)
     fill(d0k(), 28, -1)
     fill(tk(), 28, 5000)
-    fill(rst(), 36, -2.0 * BIG)
+    fill(rst(), 72, -2.0 * BIG)
     fill(d0p(), 72, 1)
     fill(keep4(), 32, 1)
-    fill(keep(0, 96, 16), 6, 0)
+    fill(keep(0, 48, 16), 3, 0)
     fill(d0k(0, 28, 14), 2, 5000)
     fill(d0k(12, 28, 14), 2, V)
-    fill(rst(0, 36, 12), 3, 2.0 * BIG)
-    for h in range(2):
-        fill(d0p(36 * h + 1, 36 * h + 4), 3, 16)
+    fill(rst(0, 72, 12), 6, 2.0 * BIG)
+    fill(d0p(1, 72, 36), 2, 16)
+    fill(d0p(2, 72, 36), 2, 17)
     fill(d0p(0, 72, 36), 2, 0)
     fill(keep4(0, 32, 4), 8, 0)
     fill(ones(), 2, 1)
@@ -211,14 +230,15 @@ def rank_program(g, core, T, topo):
     act(whole("DS"), ind(whole("D16"), vw("ql", 0, 12)))
     for b in range(4):
         quant(vw("QE", 128 * b, 128 * b + 128), vw("SE", 128 * b, 128 * b + 128), vw("F1", 3 - b, 515 - b))
-    for k in range(2):
-        cp(E0[0](k, 4, 2), vw("HG", 0, 2))
-        tt(EM[0](k, 4, 2), vw("HG", 0, 2), vw("HG", 2, 4), Op.add)
+    cp(E0[0](0, 4, 2), vw("HG", 0, 2))
+    tt(EM[0](0, 4, 2), vw("HG", 0, 2), vw("HG", 2, 4), Op.add)
 
     pen = al(72)
+    HH, NE = [al(4) for r in range(R)], [al(2) for r in range(R)]
 
     def pens(r):
-        b0, b2, uu, ub, ba, bb, ab, h1, h2, pr = al(2), al(2), al(2), al(2), al(2), al(2), al(24), al(2), al(2), al(2)
+        b0, b2, uu, ub, ba, bb, ab, pr, sg = al(2), al(2), al(2), al(2), al(2), al(2), al(24), al(2), al(2)
+        h1, h2 = HH[r], lambda a=0, b=2: HH[r](2 + a, 2 + b)
         e0, e1 = E0[r](0, 4, 2), EM[r](0, 4, 2)
         e0h = lambda h: E0[r](2 * h, 2 * h + 1)
         act(uu(), e1, scale=-1.0, bias=1.0)
@@ -235,47 +255,45 @@ def rank_program(g, core, T, topo):
             act(ab(12 * h, 12 * h + 12), ycol, Act.Abs, 2.0, ba(h, h + 1))
             act(pr(h, h + 1), e0h(h), scale=h1(h, h + 1))
         for h in range(2):
-            act(pen(h, 24, 2), ycol, Act.Relu, BIG, b0(h, h + 1))
-            act(pen(48 + h, 72, 2), ycol, Act.Relu, -BIG, b2(h, h + 1))
+            act(pen(12 * h, 12 * h + 12), ycol, Act.Relu, BIG, b0(h, h + 1))
+            act(pen(48 + 12 * h, 60 + 12 * h), ycol, Act.Relu, -BIG, b2(h, h + 1))
         for h in range(2):
-            act(pen(24 + h, 48, 2), ab(12 * h, 12 * h + 12), Act.Relu, BIG / 2, bb(h, h + 1))
-            act(pkin(36 * h, 36 * h + 1), pr(h, h + 1), Act.Sign, h2(h, h + 1))
+            act(pen(24 + 12 * h, 36 + 12 * h), ab(12 * h, 12 * h + 12), Act.Relu, BIG / 2, bb(h, h + 1))
+            act(sg(h, h + 1), pr(h, h + 1), Act.Sign, h2(h, h + 1))
+        act(NE[r](), sg(), scale=4096.0)
 
-    df, t24, i24, yy, g24, t25 = al(24), al(24), al(24), al(48), al(24), al(24)
+    df, t24, i24, yy, g24, t25, y1 = al(24), al(24), al(24), al(72), al(24), al(24), al(24)
     ii = al(24, "wi")
     du, itu = al(24, "wu"), al(24, "wu")
-    later = [lambda: cp(df(), whole("DG")),
-             lambda: cp(ii(), t24()),
-             lambda: ts(g24(), ii(), 16.0, Op.is_ge, 16.0, Op.mult),
-             lambda: ts(i24(), ii(), -float(V), Op.mult),
-             lambda: tt(t25(), g24(), ii(), Op.add),
-             lambda: tt(yy(0, 24), df(), i24(), Op.add),
-             lambda: ts(itu(), t25(), pf(3, 4), Op.add),
-             lambda: tt(yy(24, 48), df(), i24(), Op.add),
-             lambda: ts(mq(), i4(), pf(1, 2), Op.is_equal),
-             lambda: quant(whole("QV"), whole("SV"), whole("Vt"))]
-
-    def meanwhile(n=1):
-        for k in range(min(n, len(later))):
-            later.pop(0)()
-
     cp(du(), whole("DG"))
     ts(t24(), whole("DG"), -5.5, Op.add, 1.0 / V, Op.mult)
+    cp(df(), whole("DG"))
+    cp(ii(), t24())
+    ts(g24(), ii(), 16.0, Op.is_ge, 16.0, Op.mult)
+    ts(i24(), ii(), -float(V), Op.mult)
+    tt(t25(), g24(), ii(), Op.add)
+    tt(yy(0, 24), df(), i24(), Op.add)
+    ts(itu(), t25(), pf(3, 4), Op.add)
+    tt(yy(24, 48), df(), i24(), Op.add)
+    tt(yy(48, 72), df(), i24(), Op.add)
+    ts(y1(), yy(0, 24), 1.0, Op.add)
+    ts(mq(), i4(), pf(1, 2), Op.is_equal)
+    quant(whole("QV"), whole("SV"), whole("Vt"))
     cp(ind(whole("DINV"), du()), whole("j4"))
+    first = [None, len(ops) - 1, len(ops)]
     quant(whole("QU"), whole("SU"), whole("U"))
     ts(m64(), m64i(), pf(0, 1), Op.is_equal)
     qur = whole("QUR")
     add("v", lambda: g.vector.tensor_copy(qur[0].bitcast(dt.uint32), ind(whole("QU"), whole("uo"), True)[0]),
-        [whole("QU"), whole("uo")], [qur])
+        [ind(whole("QU"), whole("uo"), True)], [qur])
     pens(0)
     act(whole("SUR"), ind(whole("SU"), whole("uo")), Act.Copy)
 
-    mn, lp, lw, fa, t8, t4, ela = al(2), al(72), al(72), al(12), al(8), al(4), al(4)
-    m01, c10, nb, dd, dn, pko = al(2), al(2), al(2), al(4), al(4), al(72)
-    tko = al(28)
+    mn, lp, lw, fa, t4 = al(2), al(72), al(72), al(12), al(4)
+    m01, c10, dd, dn, pko, tko = al(2), al(2), al(4), al(4), al(72), al(28)
+    ek, xy, cb, ca, nt, di, pr2, up, pp, sm = al(2), al(4), al(2), al(2), al(48), al(48), al(48), al(24), al(24), al(24)
     pk, ff = al(24, "wi"), al(96, "wi")
-    nm1, uz, gg, gd, t1, o0, isb, t3, un, em = al(24), al(72), al(72), al(24), al(24), al(24), al(24), al(24), al(24), al(48)
-    t5, t6, phm, phs = al(24), al(24), al(32), al(32)
+    gg, un, em, t5, t6, phm, phs = al(72), al(24), al(48), al(24), al(24), al(32), al(32)
     eng8 = topo.engines(core, nxt)
     half = len(eng8) // 2
     masks = [sum(1 << e for e in eng8[:half]), sum(1 << e for e in eng8[half:])]
@@ -295,31 +313,27 @@ def rank_program(g, core, T, topo):
         halves(r, "QUR", "SUR", 0)
         for t in range(4):
             act(plane(t), vw(X, t, 4 * C, 4), scale=0.5)
-        meanwhile(2)
         for h in range(2):
             for k in range(3):
-                a = 128 * k + 64 * h
+                a = HC * h + 64 * k
                 tt(vw("MK", a, a + 64), vw("ps", 512 * h + k, 512 * h + HC, 3), m64(), Op.mult)
-        meanwhile()
-        for k in range(4):
-            scan(vw("SS", 96 * k, 96 * k + 96), keep(), vw("MK", k, C, 4), 0.0, Op.mult, Op.add)
-        meanwhile()
         for h in range(2):
-            least(mn(h, h + 1), vw("SS", 16 * h + 15, C, 32))
-        tt(lp(0, 24), vw("SS", 15, C, 16), pen(0, 24), Op.add)
+            for k in range(4):
+                a = HC * h + 48 * k
+                scan(vw("SS", a, a + 48), keep(), vw("MK", HC * h + k, HC * h + HC, 4), 0.0, Op.mult, Op.add)
         for h in range(2):
-            ts(tk(14 * h, 14 * h + 12), vw("SS", 16 * h + 15, C, 32), mn(h, h + 1), Op.is_gt, 1000.0, Op.mult)
-        tt(lp(24, 48), vw("SS", 15, C, 16), pen(24, 48), Op.add)
+            sh = vw("SS", HC * h + 15, HC * h + HC, 16)
+            least(mn(h, h + 1), sh)
+            ts(tk(14 * h, 14 * h + 12), sh, mn(h, h + 1), Op.is_gt, 1000.0, Op.mult)
+        for s in range(3):
+            tt(lp(24 * s, 24 * s + 24), vw("SS", 15, C, 16), pen(24 * s, 24 * s + 24), Op.add)
         scan(tko(), d0k(), tk(), 0.0, Op.add, Op.min)
-        tt(lp(48, 72), vw("SS", 15, C, 16), pen(48, 72), Op.add)
         cp(ku(), tko(13, 28, 14))
         for t in range(4):
             act(vw("AG", t, 128, 4), ind(plane(t), ku()), scale=2.0)
-        for h in range(2):
-            scan(lw(36 * h, 36 * h + 36), rst(), lp(h, 72, 2), 0.0, Op.max, Op.min)
-        k1 = lambda h: tko(14 * h + 12, 14 * h + 13)
+        scan(lw(), rst(), lp(), 0.0, Op.max, Op.min)
         k12 = tko(12, 28, 14)
-        low = lambda s: lw(11 + 12 * s, 72, 36)
+        low = lambda s: lw(24 * s + 11, 24 * s + 24, 12)
         tt(fa(1, 4, 2), k12, E0[r](0, 4, 2), Op.is_gt)
         tt(m01(), low(0), low(1), Op.max)
         tt(c10(), low(1), low(0), Op.is_gt)
@@ -339,37 +353,36 @@ def rank_program(g, core, T, topo):
                 local_sem=T.sem["out%d" % r])
         add("g", send, [qa, sa], [], "r", T.sem["out%d" % r], 2 * half)
         add("x", None, [], [lq, ls], "x", T.sem["arr%d" % r], 2 * half)
+        if r == 0:
+            first[0] = len(ops) - 1
         lqv, lsv = vw("LQ%d" % r, 32, 160), vw("LS%d" % r, 32, 160)
         for b in range(8):
             e = 128 * (b % 4)
             mm(b, 128, vw("QE", e, e + 128), vw("SE", e, e + 128), lqv, lsv, True, b < 4)
-        tt(t8(), fa(0, 8), EM[r](), Op.mult)
-        tt(fa(8, 12), fa(0, 4), fa(4, 8), Op.max)
-        tt(t4(), t8(0, 4), t8(4, 8), Op.max)
-        tt(dd(), fa(5, 12, 2), fa(4, 12, 2), Op.subtract)
-        tt(ela(), t4(), E0[r](), Op.max)
-        meanwhile()
-        tt(pkin(1, 72, 36), ela(1, 4, 2), k12, Op.subtract)
-        meanwhile()
         nn = lambda h: pkin(36 * h + 1, 36 * h + 2)
+        tt(pkin(2, 72, 36), k12, NE[r](), Op.add)
+        tt(ek(), E0[r](0, 4, 2), k12, Op.subtract)
+        tt(xy(), fa(1, 8, 2), HH[r](), Op.mult)
+        tt(t4(), fa(0, 8, 2), EM[r](0, 8, 2), Op.mult)
+        tt(cb(), fa(4, 8, 2), fa(1, 4, 2), Op.is_ge)
         for h in range(2):
-            ts(nb(h, h + 1), ela(2 * h, 2 * h + 1), k1(h), Op.is_ge, nn(h), Op.mult)
-        for h in range(2):
-            ts(pkin(36 * h + 2, 36 * h + 4), ela(2 * h, 2 * h + 2), nb(h, h + 1), Op.subtract)
-        ts(lh(0, 1), pkin(3, 4), d0k(13, 14), Op.add)
+            ts(nn(h), xy(h, h + 1), xy(2 + h, 3 + h), Op.add, ek(h, h + 1), Op.add)
+            ts(pkin(36 * h, 36 * h + 1), t4(h, h + 1), t4(2 + h, 3 + h), Op.max, E0[r](2 * h, 2 * h + 1), Op.max)
+            ts(pkin(36 * h + 3, 36 * h + 4), cb(h, h + 1), nn(h), Op.mult, -273.0, Op.mult)
+            ts(ca(h, h + 1), cb(h, h + 1), 0.0, Op.is_equal, nn(h), Op.mult)
+            ts(lh(h, h + 1), ca(h, h + 1), tko(14 * h + 13, 14 * h + 14), Op.add)
+        tt(fa(8, 12), fa(0, 4), fa(4, 8), Op.max)
+        tt(dd(), fa(5, 12, 2), fa(4, 12, 2), Op.subtract)
         for h in range(2):
             act(dn(h, 4, 2), dd(h, 4, 2), scale=nn(h))
         for h in range(2):
             act(EM[r + 1](2 * h, 2 * h + 2), ones(), scale=dn(h, h + 1), bias=EM[r](2 * h, 2 * h + 1))
             act(E0[r + 1](2 * h, 2 * h + 2), ones(), scale=dn(2 + h, 3 + h), bias=E0[r](2 * h, 2 * h + 1))
         scan(pko(), d0p(), pkin(), 0.0, Op.mult, Op.add)
-        ts(lh(1, 2), pkin(39, 40), d0k(27, 28), Op.add)
         for h in range(2):
             turn(vw("TR", 32 * h, 32 * h + 32), pko(36 * h + 4, 36 * h + 36))
-        meanwhile()
         act(vw("PM", HC, C), ind(whole("TR"), itu(12, 24)))
         cp(vw("PM", 0, HC), ind(whole("TR"), itu(0, 12)))
-        meanwhile()
         for h in range(2):
             scan(vw("PS", HC * h, HC * h + HC), whole("DS"), vw("PM", HC * h, HC * h + HC), 0.0, Op.mult, Op.add)
         if r + 1 < R:
@@ -379,48 +392,41 @@ def rank_program(g, core, T, topo):
             act(vw("TH", 4, 6), EM[R](0, 4, 2), scale=-1.0, bias=float(V))
             for h in range(2):
                 act(vw("TH", 2 + h, 3 + h), E0[R](2 * h, 2 * h + 1), scale=-1.0, bias=EM[R](2 * h, 2 * h + 1))
-        meanwhile()
         ts(pk(), vw("PS", 15, C, 16), sc(), Op.mult, 2.0 ** 23, Op.add)
         tt(phm(), ind(whole("DINV"), lh()), mq(), Op.mult)
-        fn_, fne = ff(48, 72), ff(72, 96)
         ts(ff(0, 24), pk(), 15, Op.bitwise_and)
-        ts(ff(24, 48), pk(), 4, Op.logical_shift_right, 15, Op.bitwise_and)
-        ts(fn_, pk(), 8, Op.logical_shift_right, 15, Op.bitwise_and)
-        tt(uz(0, 48), yy(), ff(0, 48), Op.subtract)
-        ts(nm1(), fn_, -1.0, Op.add)
-        ts(gg(0, 48), uz(0, 48), 0.0, Op.is_ge)
-        tt(uz(48, 72), nm1(), uz(24, 48), Op.subtract)
-        tt(gd(), gg(0, 24), gg(24, 48), Op.subtract)
-        ts(gg(48, 72), uz(48, 72), 0.0, Op.is_ge)
-        tt(t3(), uz(48, 72), uz(0, 24), Op.subtract)
-        tt(isb(), gg(24, 48), gg(48, 72), Op.mult)
-        tt(t1(), gd(), fn_, Op.mult)
-        tt(t5(), t3(), isb(), Op.mult)
-        tt(o0(), t1(), df(), Op.add)
-        ts(fne, pk(), 12, Op.logical_shift_right, 1, Op.bitwise_and)
-        tt(em(0, 24), o0(), t5(), Op.add)
-        tt(un(), uz(0, 24), fne, Op.mult)
+        ts(ff(24, 48), pk(), 8, Op.logical_shift_right, 15, Op.bitwise_and)
+        ts(ff(48, 72), pk(), 4, Op.logical_shift_right, 15, Op.bitwise_and)
+        ts(ff(72, 96), pk(), 12, Op.logical_shift_right, 1, Op.bitwise_and)
+        tt(gg(), yy(), ff(0, 72), Op.is_ge)
+        tt(nt(0, 24), ff(48, 72), ff(24, 48), Op.subtract)
+        tt(up(), ff(0, 24), yy(0, 24), Op.subtract)
+        tt(pp(), ff(48, 72), y1(), Op.subtract)
+        tt(di(), gg(0, 48), gg(24, 72), Op.subtract)
+        tt(nt(24, 48), pp(), up(), Op.add)
+        tt(pr2(), di(), nt(), Op.mult)
+        tt(un(), up(), ff(72, 96), Op.mult)
+        tt(sm(), pr2(0, 24), pr2(24, 48), Op.add)
+        tt(t6(), un(), di(24, 48), Op.mult)
+        tt(em(0, 24), sm(), df(), Op.add)
+        tt(t5(), df(), t6(), Op.subtract)
         cp(lu(0, 24), em(0, 24))
-        tt(t6(), un(), isb(), Op.mult)
-        scan(phs(), keep4(), phm(), 0.0, Op.mult, Op.add)
-        tt(em(24, 48), em(0, 24), t6(), Op.add)
-        ts(ph(), phs(3, 32, 4), pf(2, 3), Op.add)
+        tt(em(24, 48), sm(), t5(), Op.add)
         cp(lu(24, 48), em(24, 48))
-        meanwhile(9)
+        scan(phs(), keep4(), phm(), 0.0, Op.mult, Op.add)
+        ts(ph(), phs(3, 32, 4), pf(2, 3), Op.add)
         if r == R - 1:
             turn(whole("TT"), whole("TH"))
             for k in range(8):
                 a, p = k // 2, k % 2
                 dma("y", T.oh[k, :], T.TT[32 * a:32 * a + 6, 16 * p:16 * p + 16], [whole("TT")], [])
-
+        for b in range(4):
+            act(vw("AG", 512 + b, 640, 4), vw("ps", 512 * b + 96, 512 * b + 128), scale=2.0 ** -6)
+        quant(whole("QG"), whole("SG"), gtile)
+        for b in range(4):
+            e = 128 * b
+            mm(4 + b, 128, vw("WQ", e, e + 128), vw("WS", e, e + 128), whole("QG"), whole("SG"), False, True)
         for t in range(4):
-            if t == 2:
-                for b in range(4):
-                    act(vw("AG", 512 + b, 640, 4), vw("ps", 512 * b + 96, 512 * b + 128), scale=2.0 ** -6)
-                quant(whole("QG"), whole("SG"), gtile)
-                for b in range(4):
-                    e = 128 * b
-                    mm(4 + b, 128, vw("WQ", e, e + 128), vw("WS", e, e + 128), whole("QG"), whole("SG"), False, True)
             for h in range(2):
                 t1v = vw("T1", C * t + HC * h, C * t + HC * h + HC)
                 act(t1v, ind(plane(t), lu(12 * h, 12 * h + 12)))
@@ -440,13 +446,10 @@ def rank_program(g, core, T, topo):
     for k in range(4):
         dma("y", T.osc[4 * k:4 * k + 4, :], T["SX%d" % R][32 * k:32 * k + 4, :], [whole("SX%d" % R)], [])
 
-    qsem = {"v": T.sem.qv, "s": T.sem.qs, "t": T.sem.qt, "g": T.sem.qg}
-    count = {"v": 0, "s": 0, "t": 0, "g": 0}
-    know = {q: {} for q in eng}
-    hist = {}
+    hist, last = {}, {}
 
     def banks(m):
-        return [k for k in range(8) if (m >> (512 * k)) & ((1 << 512) - 1)]
+        return set(k for k in range(8) if (m >> (512 * k)) & ((1 << 512) - 1))
 
     for i, o in enumerate(ops):
         q = o["q"]
@@ -455,7 +458,7 @@ def rank_program(g, core, T, topo):
             for j, mj, wj in hist.get(name, []):
                 p = ops[j]
                 if name == "ps" and p["q"] != q:
-                    if set(banks(m)) & set(banks(mj)):
+                    if banks(m) & banks(mj):
                         need.add(j)
                 elif (m & mj) and (wr or wj) and not (q == "t" and p["q"] == "t"):
                     need.add(j)
@@ -463,6 +466,67 @@ def rank_program(g, core, T, topo):
             hist.setdefault(name, []).append((i, m, False))
         for name, m in o["w"]:
             hist.setdefault(name, []).append((i, m, True))
+        o["need"] = need
+        o["after"] = [last[q]] if q in "tgy" and q in last else []
+        if q == "x":
+            o["need"], o["after"] = set(), [i - 1]
+        last[q] = i
+        o["lat"] = {"c": 0.0, "d": 2.5, "r": 0.0, "x": FLIGHT}[o["kind"]]
+    for i, lat in enumerate((1.9, 1.9, 2.6, 3.4, 3.9)):
+        ops[i]["lat"] = lat
+    ops[first[0]]["lat"] += 1.5
+    ops[first[2]]["after"] = [first[1]]
+
+    for o in ops:
+        o["tail"] = o["cost"] + o["lat"]
+    for i in range(len(ops) - 1, -1, -1):
+        o = ops[i]
+        for j in list(o["need"]) + o["after"]:
+            p = ops[j]
+            p["tail"] = max(p["tail"], p["cost"] + p["lat"] + (WAKE if j in o["need"] else 0.0) + o["tail"])
+    free = {q: 0.0 for q in "vstgyx"}
+    left = list(range(len(ops)))
+    order = []
+    while left:
+        pick = None
+        for q in free:
+            ready = []
+            for i in left:
+                o = ops[i]
+                if o["q"] == q and all("end" in ops[j] for j in list(o["need"]) + o["after"]):
+                    s = max([free[q]] + [ops[j]["end"] + WAKE for j in o["need"]] + [ops[j]["end"] - ops[j]["lat"] for j in o["after"]])
+                    ready.append((o["tail"], -i, s))
+            if not ready:
+                continue
+            best = max(ready)
+            fit = [x for x in ready if x[2] + ops[-x[1]]["cost"] <= best[2] + SLACK and x[2] < best[2]]
+            if fit:
+                soon = min(x[2] for x in fit)
+                best = max(x for x in fit if x[2] <= soon + 0.01)
+            if pick is None or best[2] < pick[2]:
+                pick = best
+        o = ops[-pick[1]]
+        free[o["q"]] = pick[2] + o["cost"]
+        o["end"] = free[o["q"]] + o["lat"]
+        left.remove(-pick[1])
+        order.append(-pick[1])
+
+    qsem = {"v": T.sem.qv, "s": T.sem.qs, "t": T.sem.qt, "g": T.sem.qg}
+    count = {"v": 0, "s": 0, "t": 0, "g": 0}
+    know = {q: {} for q in eng}
+    place = {i: k for k, i in enumerate(order)}
+
+    def wait(q, p):
+        kn = know[q]
+        if kn.get(p["key"], 0) < p["cnt"]:
+            eng[q].wait_ge(p["sem"], p["cnt"])
+            for k, c in p["clock"].items():
+                if kn.get(k, 0) < c:
+                    kn[k] = c
+
+    for i in order:
+        o = ops[i]
+        q = o["q"]
         if o["kind"] == "c":
             count[q] += 1
             o["key"], o["sem"], o["cnt"] = q, qsem[q], count[q]
@@ -471,25 +535,14 @@ def rank_program(g, core, T, topo):
         if o["kind"] == "x":
             o["clock"] = {i: o["cnt"]}
             continue
-        kn = know[q]
-        for j in sorted(need, reverse=True):
-            p = ops[j]
-            if kn.get(p["key"], 0) < p["cnt"]:
-                eng[q].wait_ge(p["sem"], p["cnt"])
-                for k, c in p["clock"].items():
-                    if kn.get(k, 0) < c:
-                        kn[k] = c
+        for j in sorted(o["need"], key=lambda j: -place[j]):
+            wait(q, ops[j])
         ins = o["fn"]()
         if o["kind"] == "c":
             ins.then_inc(o["sem"], 1)
         elif o["kind"] == "d":
             ins.then_inc(o["sem"], 16)
-        o["clock"] = dict(kn)
+        o["clock"] = dict(know[q])
         o["clock"][o["key"]] = o["cnt"]
-    kn = know["g"]
-    for o in reversed(ops):
-        if kn.get(o["key"], 0) < o["cnt"]:
-            g.wait_ge(o["sem"], o["cnt"])
-            for k, c in o["clock"].items():
-                if kn.get(k, 0) < c:
-                    kn[k] = c
+    for i in reversed(order):
+        wait("g", ops[i])

from concourse.bass import DstId, RemoteDMATransfer
from concourse.mybir import dt, AluOpType, AxisListType, ActivationFunctionType

C, V, B, R = 384, 12, 32, 3
HC = C // 2
BIG = 2.0 ** 98
UP = 2.0 ** 19
WAKE, SLACK, FLIGHT = 0.17, 0.03, 4.3
Q4, U8 = "float8_e4m3fn_x4", "uint8"

SCRATCH = {"ps": ("psum", [128, 4096], "float32")}


def _buf(name, n, dtype):
    SCRATCH[name] = ("sbuf", [128, n], dtype)


for _r in range(R + 1):
    _buf("X%d" % _r, 4 * C, "bfloat16")
    _buf("QX%d" % _r, C, Q4)
    _buf("SX%d" % _r, C, U8)
for _r in range(R):
    _buf("QA%d" % _r, 128, Q4)
    _buf("SA%d" % _r, 128, U8)
    _buf("LQ%d" % _r, 160, Q4)
    _buf("LS%d" % _r, 256, U8)
for _n, _w, _d in [
        ("XH", 4 * C, "bfloat16"),
        ("T1", 4 * C, "bfloat16"), ("U", 512, "bfloat16"), ("Vt", 512, "bfloat16"), ("QU", 128, Q4), ("SU", 128, U8),
        ("QUR", 128, Q4), ("SUR", 128, U8), ("QV", 128, Q4), ("SV", 128, U8), ("WQ", 512, Q4), ("WS", 512, U8),
        ("F0", 520, "bfloat16"), ("F1", 520, "bfloat16"), ("QE", 512, Q4), ("SE", 512, U8), ("AG", 640, "bfloat16"),
        ("QG", 128, Q4), ("SG", 128, U8), ("H", 128, "bfloat16"),
        ("HG", 8, "int32"), ("DG", 24, "int32"), ("ci", 16, "int32"), ("uo", 8, "uint16"), ("cf", 512, "float32"),
        ("D16", 16, "float32"), ("DS", HC, "float32"), ("ql", 24, "uint16"),
        ("j4", C, "float32"), ("DINV", C, "float32"), ("TR", 64, "float32"), ("MK", C, "float32"), ("SS", C, "float32"),
        ("PM", C, "float32"), ("PS", C, "float32"), ("w", 2048, "float32"), ("wi", 256, "int32"), ("wu", 256, "uint16"),
        ("TH", 32, "float32"), ("TT", 32, "float32"), ("Y", C, "float32")]:
    _buf(_n, _w, _d)

NDMA = 40
SEMAPHORES = ["qv", "qs", "qt", "qg"] + ["d%d" % i for i in range(NDMA)] + \
             ["arr%d" % r for r in range(R)] + ["out%d" % r for r in range(R)]

Op, Act = AluOpType, ActivationFunctionType


def rank_program(g, core, T, topo):
    rank = T.rank_of(core)
    if rank is None:
        return
    nxt = T.cores[(rank + 1) % len(T.cores)]
    ops = []
    eng = {"v": g.vector, "s": g.scalar, "t": g.tensor, "g": g, "y": g.sync}

    def vw(name, a, b, s=1):
        m = 0
        for c in range(a, b, s):
            m |= 1 << c
        ap = T[name][:, a:b] if s == 1 else T[name][:, a:b:s]
        return (ap, name, m)

    def ind(win, off, words=False):
        ap = win[0].bitcast(dt.uint32) if words else win[0]
        return (ap.indirect(off[0]), win[1], win[2], off)

    def acc(views):
        out = []
        for x in views:
            if isinstance(x, tuple):
                out.append((x[1], x[2]))
                if len(x) == 4:
                    out.append((x[3][1], x[3][2]))
        return out

    def ap(x):
        return x[0] if isinstance(x, tuple) else x

    def cost(q, kind, reads, writes):
        if kind != "c":
            return 0.1
        o = writes[0]
        n = bin(o[2]).count("1")
        if len(o) == 4:
            return 0.05 + 0.048 * bin(o[3][2]).count("1")
        if q == "t":
            return 0.0008 * (n + 16)
        if q == "g":
            return 0.15 + 0.002 * n
        if any(isinstance(x, tuple) and len(x) == 4 for x in reads):
            return 0.05 + 0.0015 * n
        if len(writes) == 2:
            return 0.015 + 0.00105 * n
        return max(0.064, 0.001 * n)

    def add(q, fn, reads, writes, kind="c", sem=None, cnt=0):
        rd = acc(reads) + [(x[3][1], x[3][2]) for x in writes if len(x) == 4]
        ops.append({"q": q, "fn": fn, "cost": cost(q, kind, reads, writes), "r": rd, "w": [(x[1], x[2]) for x in writes],
                    "kind": kind, "sem": sem, "cnt": cnt})

    def tt(out, a, b, op):
        add("v", lambda: g.vector.tensor_tensor(out[0], a[0], b[0], op), [a, b], [out])

    def ts(out, a, s1, op0, s2=None, op1=None):
        if op1 is None:
            add("v", lambda: g.vector.tensor_scalar(out[0], a[0], ap(s1), None, op0), [a, s1], [out])
        else:
            add("v", lambda: g.vector.tensor_scalar(out[0], a[0], ap(s1), ap(s2), op0, op1), [a, s1, s2], [out])

    def cp(out, a):
        add("v", lambda: g.vector.tensor_copy(out[0], a[0]), [a], [out])

    def scan(out, d0, d1, init, op0, op1):
        add("v", lambda: g.vector.tensor_tensor_scan(out[0], d0[0], d1[0], init, op0, op1), [d0, d1], [out])

    def ms(out, val):
        add("v", lambda: g.vector.memset(out[0], val), [], [out])

    def quant(q, s, x):
        add("v", lambda: g.vector.quantize_mx(q[0], s[0], x[0]), [x], [q, s])

    def turn(out, a):
        add("v", lambda: g.vector.transpose(out[0], a[0]), [a], [out])

    def least(out, a):
        add("v", lambda: g.vector.tensor_reduce(out[0], a[0], AxisListType.X, Op.min), [a], [out])

    def act(out, a, func=Act.Identity, scale=1.0, bias=None):
        if func == Act.Copy:
            add("s", lambda: g.scalar.activation(out[0], a[0], func), [a], [out])
        elif bias is None:
            add("s", lambda: g.scalar.activation(out[0], a[0], func, scale=ap(scale)), [a, scale], [out])
        else:
            add("s", lambda: g.scalar.activation(out[0], a[0], func, bias=ap(bias), scale=ap(scale)), [a, scale, bias], [out])

    def mm(bank, n, wq, ws, xq, xs, start=True, stop=True):
        out = vw("ps", 512 * bank, 512 * bank + n)
        add("t", lambda: g.tensor.matmul_mx(out[0], wq[0], ws[0], xq[0], xs[0], start, stop), [wq, ws, xq, xs], [out])

    def iota(out, pattern, base, cm=0, small=True):
        if small:
            add("g", lambda: g.iota(out[0], pattern, base, cm, allow_small_or_imprecise_dtypes=True), [], [out])
        else:
            add("g", lambda: g.iota(out[0], pattern, base, cm), [], [out])

    ndma = [0]

    def dma(q, out, in_, reads, writes):
        sem = T.sem["d%d" % ndma[0]]
        ndma[0] += 1
        add(q, lambda: eng[q].dma_start(out, in_), reads, writes, "d", sem, 16)

    top = {"w": 0, "wi": 0, "wu": 0, "cf": 0}

    def al(n, name="w"):
        a = top[name]
        top[name] = a + n + n % 2
        return lambda lo=0, hi=n, s=1: vw(name, a + lo, a + hi, s)

    def whole(name):
        return vw(name, 0, SCRATCH[name][1][1])

    def bytes_of(x):
        return x[0].bitcast(dt.uint8)

    dma("s", T.HG[:, 0:6], T.hg[:], [], [whole("HG")])
    dma("s", T.DG[:], T.dg[:], [], [whole("DG")])
    dma("y", T.U[:], T.u[:], [], [whole("U")])
    for h in range(2):
        dma("y", T.X0[:, 4 * HC * h:4 * HC * (h + 1)], T.x[:, 4 * HC * h:4 * HC * (h + 1)], [], [vw("X0", 4 * HC * h, 4 * HC * (h + 1))])

    pint, uoi, pti = vw("ci", 0, 1), vw("ci", 8, 16), lambda k: vw("ci", k, k + 1)
    yc, i4, mq, keep4, keep, m64, m64i = al(26, "cf"), al(32, "cf"), al(32, "cf"), al(32, "cf"), al(48, "cf"), al(64, "cf"), al(64)
    pf, d0k, rst, ones, d0p, sc = al(4, "cf"), al(28, "cf"), al(72, "cf"), al(2, "cf"), al(72, "cf"), al(1, "cf")
    ycol = yc(1, 13)
    tk, pkin, da, db = al(28), al(72), al(16), al(16)
    EM, E0 = [al(8) for r in range(R + 1)], [al(4) for r in range(R + 1)]
    atile, gtile = vw("AG", 0, 512), vw("AG", 128, 640)

    def fill(out, n, val):
        act(out, vw("F0", 0, n), scale=0.0, bias=float(val))

    ms(whole("F0"), 64.0)
    iota(pint, [[0, 1]], 0, 1, False)
    iota(uoi, [[16, 8]], 0, 0, False)
    iota(yc(), [[1, 26]], -1)
    iota(whole("j4"), [[4, C]], 0)
    iota(m64i(), [[1, 16], [0, 4]], 0)
    add("g", lambda: g.affine_select(T.F1[:], T.F0[:], [[-1, 520]], Op.is_equal, 0.0, 3, 4), [whole("F0")], [whole("F1")])
    iota(i4(), [[0, 8], [1, 4]], 0)
    iota(whole("TH"), [[0, 32]], 0)
    fill(pkin(), 72, 0)
    fill(keep(), 48, 1)
    fill(d0k(), 28, -1)
    fill(tk(), 28, 5000)
    fill(rst(), 72, -2.0 * BIG)
    fill(d0p(), 72, 1)
    fill(keep4(), 32, 1)
    fill(keep(0, 48, 16), 3, 0)
    fill(d0k(0, 28, 14), 2, 5000)
    fill(d0k(12, 28, 14), 2, V)
    fill(rst(0, 72, 12), 6, 2.0 * BIG)
    fill(d0p(1, 72, 36), 2, 16)
    fill(d0p(2, 72, 36), 2, 17)
    fill(d0p(0, 72, 36), 2, 0)
    fill(keep4(0, 32, 4), 8, 0)
    fill(ones(), 2, 1)
    for r in range(R):
        fill(EM[r](4, 8), 4, V)
    ms(gtile, 0.0)
    ts(pti(1), pint, 15, Op.bitwise_and)
    ts(pti(2), pint, 2, Op.logical_shift_right, 3, Op.bitwise_and)
    ts(pti(3), pint, 3, Op.bitwise_and)
    ts(pti(4), pint, 16, Op.bitwise_and)
    cp(whole("uo"), uoi)
    cp(pf(), vw("ci", 1, 5))
    quant(vw("LQ0", 0, 128), vw("LS0", 0, 128), gtile)
    dma("y", bytes_of(whole("WQ")), T.wc[:], [], [whole("WQ")])
    dma("y", T.WS[:], T.ws[:], [], [whole("WS")])
    for r in range(1, R):
        dma("y", bytes_of(vw("LQ%d" % r, 0, 128)), bytes_of(vw("LQ0", 0, 128)), [vw("LQ0", 0, 128)], [vw("LQ%d" % r, 0, 128)])
        dma("y", vw("LS%d" % r, 0, 128)[0], vw("LS0", 0, 128)[0], [vw("LS0", 0, 128)], [vw("LS%d" % r, 0, 128)])
    dma("y", T.Vt[:], T.v[:], [], [whole("Vt")])
    ts(da(), yc(1, 17), pf(0, 1), Op.not_equal)
    ts(db(), yc(0, 16), pf(0, 1), Op.is_equal, UP - 1.0, Op.mult)
    ts(whole("ql"), yc(0, 24), 0.0, Op.mult, pf(0, 1), Op.add)
    ts(sc(), pf(0, 1), 15.0, Op.is_equal, 1.0 / UP, Op.max)
    tt(whole("D16"), da(), db(), Op.add)
    for h in range(2):
        ts(d0k(14 * h + 13, 14 * h + 14), pf(0, 1), float(V), Op.mult, float(HC * h - 1), Op.add)
    act(whole("DS"), ind(whole("D16"), vw("ql", 0, 12)))
    for b in range(4):
        quant(vw("QE", 128 * b, 128 * b + 128), vw("SE", 128 * b, 128 * b + 128), vw("F1", 3 - b, 515 - b))
    cp(E0[0](0, 4, 2), vw("HG", 0, 2))
    tt(EM[0](0, 4, 2), vw("HG", 0, 2), vw("HG", 2, 4), Op.add)

    pen = al(72)
    HH, NE = [al(4) for r in range(R)], [al(2) for r in range(R)]

    def pens(r):
        b0, b2, uu, ub, ba, bb, ab, pr, sg = al(2), al(2), al(2), al(2), al(2), al(2), al(24), al(2), al(2)
        h1, h2 = HH[r], lambda a=0, b=2: HH[r](2 + a, 2 + b)
        e0, e1 = E0[r](0, 4, 2), EM[r](0, 4, 2)
        e0h = lambda h: E0[r](2 * h, 2 * h + 1)
        act(uu(), e1, scale=-1.0, bias=1.0)
        act(ub(), e1, scale=-BIG / 2, bias=BIG / 2)
        act(b0(), e0, scale=-BIG, bias=BIG)
        act(b2(), e1, scale=BIG)
        act(h2(), e1, scale=-1.0, bias=float(V))
        for h in range(2):
            act(ba(h, h + 1), e0h(h), scale=-1.0, bias=uu(h, h + 1))
            act(h1(h, h + 1), e0h(h), scale=-1.0, bias=EM[r](2 * h, 2 * h + 1))
        for h in range(2):
            act(bb(h, h + 1), e0h(h), scale=BIG / 2, bias=ub(h, h + 1))
        for h in range(2):
            act(ab(12 * h, 12 * h + 12), ycol, Act.Abs, 2.0, ba(h, h + 1))
            act(pr(h, h + 1), e0h(h), scale=h1(h, h + 1))
        for h in range(2):
            act(pen(12 * h, 12 * h + 12), ycol, Act.Relu, BIG, b0(h, h + 1))
            act(pen(48 + 12 * h, 60 + 12 * h), ycol, Act.Relu, -BIG, b2(h, h + 1))
        for h in range(2):
            act(pen(24 + 12 * h, 36 + 12 * h), ab(12 * h, 12 * h + 12), Act.Relu, BIG / 2, bb(h, h + 1))
            act(sg(h, h + 1), pr(h, h + 1), Act.Sign, h2(h, h + 1))
        act(NE[r](), sg(), scale=4096.0)

    df, t24, i24, yy, g24, t25, y1 = al(24), al(24), al(24), al(72), al(24), al(24), al(24)
    ii = al(24, "wi")
    du, itu = al(24, "wu"), al(24, "wu")
    cp(du(), whole("DG"))
    ts(t24(), whole("DG"), -5.5, Op.add, 1.0 / V, Op.mult)
    cp(df(), whole("DG"))
    cp(ii(), t24())
    ts(g24(), ii(), 16.0, Op.is_ge, 16.0, Op.mult)
    ts(i24(), ii(), -float(V), Op.mult)
    tt(t25(), g24(), ii(), Op.add)
    tt(yy(0, 24), df(), i24(), Op.add)
    ts(itu(), t25(), pf(3, 4), Op.add)
    tt(yy(24, 48), df(), i24(), Op.add)
    tt(yy(48, 72), df(), i24(), Op.add)
    ts(y1(), yy(0, 24), 1.0, Op.add)
    ts(mq(), i4(), pf(1, 2), Op.is_equal)
    quant(whole("QV"), whole("SV"), whole("Vt"))
    cp(ind(whole("DINV"), du()), whole("j4"))
    first = [None, len(ops) - 1, len(ops)]
    quant(whole("QU"), whole("SU"), whole("U"))
    ts(m64(), m64i(), pf(0, 1), Op.is_equal)
    qur = whole("QUR")
    add("v", lambda: g.vector.tensor_copy(qur[0].bitcast(dt.uint32), ind(whole("QU"), whole("uo"), True)[0]),
        [ind(whole("QU"), whole("uo"), True)], [qur])
    pens(0)
    act(whole("SUR"), ind(whole("SU"), whole("uo")), Act.Copy)

    mn, lp, lw, fa, t4 = al(2), al(72), al(72), al(12), al(4)
    m01, c10, dd, dn, pko, tko = al(2), al(2), al(4), al(4), al(72), al(28)
    ek, xy, cb, ca, nt, di, pr2, up, pp, sm = al(2), al(4), al(2), al(2), al(48), al(48), al(48), al(24), al(24), al(24)
    pk, ff = al(24, "wi"), al(96, "wi")
    gg, un, em, t5, t6, phm, phs = al(72), al(24), al(48), al(24), al(24), al(32), al(32)
    eng8 = topo.engines(core, nxt)
    half = len(eng8) // 2
    masks = [sum(1 << e for e in eng8[:half]), sum(1 << e for e in eng8[half:])]
    rid, pid = topo.addr(nxt)[:2]

    def halves(r, wq, ws, bank):
        for h in range(2):
            qx, sx = vw("QX%d" % r, HC * h, HC * h + HC), vw("SX%d" % r, HC * h, HC * h + HC)
            quant(qx, sx, vw("X%d" % r, 4 * HC * h, 4 * HC * (h + 1)))
            mm(bank + h, HC, whole(wq), whole(ws), qx, sx)

    plane = lambda t: vw("XH", C * t, C * t + C)

    for r in range(R):
        X, XN = "X%d" % r, "X%d" % (r + 1)
        ku, lu, lh, ph = al(2, "wu"), al(48, "wu"), al(2, "wu"), al(8, "wu")
        halves(r, "QUR", "SUR", 0)
        for t in range(4):
            act(plane(t), vw(X, t, 4 * C, 4), scale=0.5)
        for h in range(2):
            for k in range(3):
                a = HC * h + 64 * k
                tt(vw("MK", a, a + 64), vw("ps", 512 * h + k, 512 * h + HC, 3), m64(), Op.mult)
        for h in range(2):
            for k in range(4):
                a = HC * h + 48 * k
                scan(vw("SS", a, a + 48), keep(), vw("MK", HC * h + k, HC * h + HC, 4), 0.0, Op.mult, Op.add)
        for h in range(2):
            sh = vw("SS", HC * h + 15, HC * h + HC, 16)
            least(mn(h, h + 1), sh)
            ts(tk(14 * h, 14 * h + 12), sh, mn(h, h + 1), Op.is_gt, 1000.0, Op.mult)
        for s in range(3):
            tt(lp(24 * s, 24 * s + 24), vw("SS", 15, C, 16), pen(24 * s, 24 * s + 24), Op.add)
        scan(tko(), d0k(), tk(), 0.0, Op.add, Op.min)
        cp(ku(), tko(13, 28, 14))
        for t in range(4):
            act(vw("AG", t, 128, 4), ind(plane(t), ku()), scale=2.0)
        scan(lw(), rst(), lp(), 0.0, Op.max, Op.min)
        k12 = tko(12, 28, 14)
        low = lambda s: lw(24 * s + 11, 24 * s + 24, 12)
        tt(fa(1, 4, 2), k12, E0[r](0, 4, 2), Op.is_gt)
        tt(m01(), low(0), low(1), Op.max)
        tt(c10(), low(1), low(0), Op.is_gt)
        tt(fa(5, 8, 2), k12, EM[r](0, 4, 2), Op.is_gt)
        tt(fa(4, 8, 2), low(2), m01(), Op.is_gt)
        tt(fa(0, 4, 2), c10(), fa(1, 4, 2), Op.is_ge)
        qa, sa = whole("QA%d" % r), whole("SA%d" % r)
        quant(qa, sa, atile)
        lq, ls = vw("LQ%d" % r, 128, 160), vw("LS%d" % r, 128, 256)

        def send(r=r, qa32=vw("QA%d" % r, 0, B), sa=sa, lq=lq, ls=ls):
            to = [DstId(rid=rid, pnc=pid)]
            arr = T.sem["arr%d" % r]
            return g.remote_dma_fused(
                [RemoteDMATransfer(dst_ids=to, dma_engine_mask=masks[0], remote_sem=arr, src=bytes_of(qa32), dst=bytes_of(lq)),
                 RemoteDMATransfer(dst_ids=to, dma_engine_mask=masks[1], remote_sem=arr, src=sa[0], dst=ls[0])],
                local_sem=T.sem["out%d" % r])
        add("g", send, [qa, sa], [], "r", T.sem["out%d" % r], 2 * half)
        add("x", None, [], [lq, ls], "x", T.sem["arr%d" % r], 2 * half)
        if r == 0:
            first[0] = len(ops) - 1
        lqv, lsv = vw("LQ%d" % r, 32, 160), vw("LS%d" % r, 32, 160)
        for b in range(8):
            e = 128 * (b % 4)
            mm(b, 128, vw("QE", e, e + 128), vw("SE", e, e + 128), lqv, lsv, True, b < 4)
        nn = lambda h: pkin(36 * h + 1, 36 * h + 2)
        tt(pkin(2, 72, 36), k12, NE[r](), Op.add)
        tt(ek(), E0[r](0, 4, 2), k12, Op.subtract)
        tt(xy(), fa(1, 8, 2), HH[r](), Op.mult)
        tt(t4(), fa(0, 8, 2), EM[r](0, 8, 2), Op.mult)
        tt(cb(), fa(4, 8, 2), fa(1, 4, 2), Op.is_ge)
        for h in range(2):
            ts(nn(h), xy(h, h + 1), xy(2 + h, 3 + h), Op.add, ek(h, h + 1), Op.add)
            ts(pkin(36 * h, 36 * h + 1), t4(h, h + 1), t4(2 + h, 3 + h), Op.max, E0[r](2 * h, 2 * h + 1), Op.max)
            ts(pkin(36 * h + 3, 36 * h + 4), cb(h, h + 1), nn(h), Op.mult, -273.0, Op.mult)
            ts(ca(h, h + 1), cb(h, h + 1), 0.0, Op.is_equal, nn(h), Op.mult)
            ts(lh(h, h + 1), ca(h, h + 1), tko(14 * h + 13, 14 * h + 14), Op.add)
        tt(fa(8, 12), fa(0, 4), fa(4, 8), Op.max)
        tt(dd(), fa(5, 12, 2), fa(4, 12, 2), Op.subtract)
        for h in range(2):
            act(dn(h, 4, 2), dd(h, 4, 2), scale=nn(h))
        for h in range(2):
            act(EM[r + 1](2 * h, 2 * h + 2), ones(), scale=dn(h, h + 1), bias=EM[r](2 * h, 2 * h + 1))
            act(E0[r + 1](2 * h, 2 * h + 2), ones(), scale=dn(2 + h, 3 + h), bias=E0[r](2 * h, 2 * h + 1))
        scan(pko(), d0p(), pkin(), 0.0, Op.mult, Op.add)
        for h in range(2):
            turn(vw("TR", 32 * h, 32 * h + 32), pko(36 * h + 4, 36 * h + 36))
        act(vw("PM", HC, C), ind(whole("TR"), itu(12, 24)))
        cp(vw("PM", 0, HC), ind(whole("TR"), itu(0, 12)))
        for h in range(2):
            scan(vw("PS", HC * h, HC * h + HC), whole("DS"), vw("PM", HC * h, HC * h + HC), 0.0, Op.mult, Op.add)
        if r + 1 < R:
            pens(r + 1)
        else:
            act(vw("TH", 0, 2), E0[R](0, 4, 2))
            act(vw("TH", 4, 6), EM[R](0, 4, 2), scale=-1.0, bias=float(V))
            for h in range(2):
                act(vw("TH", 2 + h, 3 + h), E0[R](2 * h, 2 * h + 1), scale=-1.0, bias=EM[R](2 * h, 2 * h + 1))
        ts(pk(), vw("PS", 15, C, 16), sc(), Op.mult, 2.0 ** 23, Op.add)
        tt(phm(), ind(whole("DINV"), lh()), mq(), Op.mult)
        ts(ff(0, 24), pk(), 15, Op.bitwise_and)
        ts(ff(24, 48), pk(), 8, Op.logical_shift_right, 15, Op.bitwise_and)
        ts(ff(48, 72), pk(), 4, Op.logical_shift_right, 15, Op.bitwise_and)
        ts(ff(72, 96), pk(), 12, Op.logical_shift_right, 1, Op.bitwise_and)
        tt(gg(), yy(), ff(0, 72), Op.is_ge)
        tt(nt(0, 24), ff(48, 72), ff(24, 48), Op.subtract)
        tt(up(), ff(0, 24), yy(0, 24), Op.subtract)
        tt(pp(), ff(48, 72), y1(), Op.subtract)
        tt(di(), gg(0, 48), gg(24, 72), Op.subtract)
        tt(nt(24, 48), pp(), up(), Op.add)
        tt(pr2(), di(), nt(), Op.mult)
        tt(un(), up(), ff(72, 96), Op.mult)
        tt(sm(), pr2(0, 24), pr2(24, 48), Op.add)
        tt(t6(), un(), di(24, 48), Op.mult)
        tt(em(0, 24), sm(), df(), Op.add)
        tt(t5(), df(), t6(), Op.subtract)
        cp(lu(0, 24), em(0, 24))
        tt(em(24, 48), sm(), t5(), Op.add)
        cp(lu(24, 48), em(24, 48))
        scan(phs(), keep4(), phm(), 0.0, Op.mult, Op.add)
        ts(ph(), phs(3, 32, 4), pf(2, 3), Op.add)
        if r == R - 1:
            turn(whole("TT"), whole("TH"))
            for k in range(8):
                a, p = k // 2, k % 2
                dma("y", T.oh[k, :], T.TT[32 * a:32 * a + 6, 16 * p:16 * p + 16], [whole("TT")], [])
        for b in range(4):
            act(vw("AG", 512 + b, 640, 4), vw("ps", 512 * b + 96, 512 * b + 128), scale=2.0 ** -6)
        quant(whole("QG"), whole("SG"), gtile)
        for b in range(4):
            e = 128 * b
            mm(4 + b, 128, vw("WQ", e, e + 128), vw("WS", e, e + 128), whole("QG"), whole("SG"), False, True)
        for t in range(4):
            for h in range(2):
                t1v = vw("T1", C * t + HC * h, C * t + HC * h + HC)
                act(t1v, ind(plane(t), lu(12 * h, 12 * h + 12)))
                tt(vw(XN, 4 * HC * h + t, 4 * HC * (h + 1), 4), ind(plane(t), lu(24 + 12 * h, 36 + 12 * h)), t1v, Op.add)
        for b in range(4):
            act(vw("H", b, 128, 4), vw("ps", 512 * (4 + b) + 96, 512 * (4 + b) + 128), scale=2.0 ** -6)
        cp(ind(whole(XN), ph()), whole("H"))

    halves(R, "QV", "SV", 2)
    for h in range(2):
        qx = vw("QX%d" % R, HC * h, HC * h + HC)
        dma("y", T.oc[:, 4 * HC * h:4 * HC * (h + 1)], bytes_of(qx), [qx], [])
    act(vw("Y", 0, HC), vw("ps", 1024, 1024 + HC))
    dma("s", T.y[:, 0:HC], T.Y[:, 0:HC], [vw("Y", 0, HC)], [])
    cp(vw("Y", HC, C), vw("ps", 1536, 1536 + HC))
    dma("s", T.y[:, HC:C], T.Y[:, HC:C], [vw("Y", HC, C)], [])
    for k in range(4):
        dma("y", T.osc[4 * k:4 * k + 4, :], T["SX%d" % R][32 * k:32 * k + 4, :], [whole("SX%d" % R)], [])

    hist, last = {}, {}

    def banks(m):
        return set(k for k in range(8) if (m >> (512 * k)) & ((1 << 512) - 1))

    for i, o in enumerate(ops):
        q = o["q"]
        need = set()
        for name, m, wr in [(n, m, False) for n, m in o["r"]] + [(n, m, True) for n, m in o["w"]]:
            for j, mj, wj in hist.get(name, []):
                p = ops[j]
                if name == "ps" and p["q"] != q:
                    if banks(m) & banks(mj):
                        need.add(j)
                elif (m & mj) and (wr or wj) and not (q == "t" and p["q"] == "t"):
                    need.add(j)
        for name, m in o["r"]:
            hist.setdefault(name, []).append((i, m, False))
        for name, m in o["w"]:
            hist.setdefault(name, []).append((i, m, True))
        o["need"] = need
        o["after"] = [last[q]] if q in "tgy" and q in last else []
        if q == "x":
            o["need"], o["after"] = set(), [i - 1]
        last[q] = i
        o["lat"] = {"c": 0.0, "d": 2.5, "r": 0.0, "x": FLIGHT}[o["kind"]]
    for i, lat in enumerate((1.9, 1.9, 2.6, 3.4, 3.9)):
        ops[i]["lat"] = lat
    ops[first[0]]["lat"] += 1.5
    ops[first[2]]["after"] = [first[1]]

    for o in ops:
        o["tail"] = o["cost"] + o["lat"]
    for i in range(len(ops) - 1, -1, -1):
        o = ops[i]
        for j in list(o["need"]) + o["after"]:
            p = ops[j]
            p["tail"] = max(p["tail"], p["cost"] + p["lat"] + (WAKE if j in o["need"] else 0.0) + o["tail"])
    free = {q: 0.0 for q in "vstgyx"}
    left = list(range(len(ops)))
    order = []
    while left:
        pick = None
        for q in free:
            ready = []
            for i in left:
                o = ops[i]
                if o["q"] == q and all("end" in ops[j] for j in list(o["need"]) + o["after"]):
                    s = max([free[q]] + [ops[j]["end"] + WAKE for j in o["need"]] + [ops[j]["end"] - ops[j]["lat"] for j in o["after"]])
                    ready.append((o["tail"], -i, s))
            if not ready:
                continue
            best = max(ready)
            fit = [x for x in ready if x[2] + ops[-x[1]]["cost"] <= best[2] + SLACK and x[2] < best[2]]
            if fit:
                soon = min(x[2] for x in fit)
                best = max(x for x in fit if x[2] <= soon + 0.01)
            if pick is None or best[2] < pick[2]:
                pick = best
        o = ops[-pick[1]]
        free[o["q"]] = pick[2] + o["cost"]
        o["end"] = free[o["q"]] + o["lat"]
        left.remove(-pick[1])
        order.append(-pick[1])

    qsem = {"v": T.sem.qv, "s": T.sem.qs, "t": T.sem.qt, "g": T.sem.qg}
    count = {"v": 0, "s": 0, "t": 0, "g": 0}
    know = {q: {} for q in eng}
    place = {i: k for k, i in enumerate(order)}

    def wait(q, p):
        kn = know[q]
        if kn.get(p["key"], 0) < p["cnt"]:
            eng[q].wait_ge(p["sem"], p["cnt"])
            for k, c in p["clock"].items():
                if kn.get(k, 0) < c:
                    kn[k] = c

    for i in order:
        o = ops[i]
        q = o["q"]
        if o["kind"] == "c":
            count[q] += 1
            o["key"], o["sem"], o["cnt"] = q, qsem[q], count[q]
        else:
            o["key"] = i
        if o["kind"] == "x":
            o["clock"] = {i: o["cnt"]}
            continue
        for j in sorted(o["need"], key=lambda j: -place[j]):
            wait(q, ops[j])
        ins = o["fn"]()
        if o["kind"] == "c":
            ins.then_inc(o["sem"], 1)
        elif o["kind"] == "d":
            ins.then_inc(o["sem"], 16)
        o["clock"] = dict(know[q])
        o["clock"][o["key"]] = o["cnt"]
    for i in reversed(order):
        wait("g", ops[i])
